import numpy as np, ml_dtypes
CORES = [66,74,82,90,194,202,210,218]
N = 8
BF = ml_dtypes.bfloat16
def gentries(a):
    return np.ascontiguousarray(a.reshape(8, 16, -1).transpose(0, 2, 1)).reshape(8, -1)
def gtable(e):
    e = np.asarray(e); return np.ascontiguousarray(e.reshape(8, -1, 16).transpose(0, 2, 1)).reshape(128, -1).astype(np.int32)
NO, D, B, K, RO, TH = 16, 4, 112, 8, 4, 9
V, NB = NO * B, NO + D
def every(z):
    return np.concatenate([z, np.stack([np.roll(z[:, :, d - 1], d, axis=0) for d in range(1, D + 1)], axis=2)], axis=2)
def parts(rng):
    a = rng.integers(0, 256, (N, 8, 15, V)); m = (rng.random((N, 8, V)) < 0.0625).astype(np.int64)
    u = np.argsort(rng.random((N, 8, NB, V)), axis=-1)[..., :16 * B].reshape(N, 8, NB, 16, B)
    e = np.argsort(rng.random((N, 8, NO, B)), axis=-1)[..., :K]
    return a, m, u, np.ascontiguousarray(e)
def firsts(e):
    z = np.zeros((N, 8, V), bool); np.put_along_axis(z, (e + B * np.arange(NO)[:, None]).reshape(N, 8, -1), True, 2)
    return z
def reach(u, e):
    z = np.zeros((N, 8, V), bool); q = np.take_along_axis(u, every(e)[:, :, :, None, :], 4)
    np.put_along_axis(z, q.reshape(N, 8, -1), True, 2)
    return z
def cover(rng):
    o = np.argsort(rng.random((N, V)), axis=-1)
    return np.stack([np.roll(o, -16 * K * c, axis=1) for c in range(NB)], axis=1)
def aim(rng, e, g, o):
    ee = every(e)[:, g]; w = np.zeros((N, NB, 16, B), np.int64)
    for r in range(N):
        for c in range(NB):
            rest = np.ones(B, bool); rest[ee[r, c]] = False
            w[r, c][:, ee[r, c]] = o[r, c, :16 * K].reshape(16, K)
            w[r, c][:, rest] = rng.permutation(o[r, c, 16 * K:])[:16 * (B - K)].reshape(16, B - K)
    return w
def pack(a, m, u, e):
    rec = np.concatenate([a, m[:, :, None]], axis=2).reshape(N, 128, V).astype(np.float32).astype(BF)
    up = np.ascontiguousarray(u.transpose(0, 1, 3, 2, 4).reshape(N, 128, NB * B)).astype(np.int32)
    return {"rec": rec, "up": up, "fr": np.stack([gtable(z.reshape(8, -1)) for z in e])}
def setup_inputs(rng):
    return pack(*parts(rng))
def setup_inputs_room(rng):
    a, m, u, e = parts(rng); c = reach(u, e); z = firsts(e); can = c & ~z; pick = np.zeros((N, 8, V), bool)
    for r in range(N):
        for g in range(8):
            for b in range(NO):
                o = b * B + rng.permutation(np.flatnonzero(can[r, g, b * B:(b + 1) * B])); n = int(rng.choice(np.array([0, 1, K - 1, K, K + 1, B])))
                if r == 0 and b == 0: n = (K, K + 1, B, K - 1, 1, 0, K, K + 1)[g]
                pick[r, g, o[:n]] = True
    a = np.where(c[:, :, None], np.where(pick[:, :, None], rng.integers(150, 256, a.shape), rng.integers(0, 51, a.shape)), a)
    a = np.where(z[:, :, None], rng.integers(100, 111, a.shape), a)
    return pack(a, z.astype(np.int64), u, e)
def setup_inputs_ties(rng):
    a, m, u, e = parts(rng); z = firsts(e)
    lo = np.array([0, 254, 100, 0, 7, 127, 1, 128]).reshape(1, 8, 1, 1); step = np.array([1, 1, 1, 255, 1, 1, 2, 1]).reshape(1, 8, 1, 1)
    p = np.where(z, 0.6, 0.15 + 0.3 * rng.random((N, 8, V)))[:, :, None]
    a = lo + step * (rng.random(a.shape) < p)
    a[:, 1] = np.where((rng.random((N, V)) < 0.6)[:, None], 255, a[:, 1])
    return pack(a, m, u, e)
def setup_inputs_meet(rng):
    a, m, u, e = parts(rng)
    u[:, ::2] = u[:, ::2, :1].copy(); e[:, ::2] = e[:1, ::2, :1].copy()
    i = 1 + np.argsort(rng.random((N, 4, NO, B - 2)), axis=-1)[..., :K - 2]
    e[:, 1::2, :, 2:] = i; e[:, 1::2, :, 0] = 0; e[:, 1::2, :, 1] = B - 1
    base = np.arange(16 * B).reshape(B, 16).T; u[:, 1] = base; u[:, 1, NO:] = base + V - 16 * B
    o = np.argsort((np.arange(V) + rng.integers(0, 16, (N, 1, 1))) % 16 + rng.random((N, 1, V)), axis=-1)
    u[:, 2] = aim(rng, e, 2, np.broadcast_to(o, (N, NB, V)))[:, :1]
    u[:, 3] = aim(rng, e, 3, cover(rng)); z = firsts(e)
    a[:, 3] = np.where(z[:, 3][:, None], rng.integers(0, 51, (N, 15, V)), rng.integers(150, 256, (N, 15, V))); m[:, 3] = 0
    return pack(a, m, u, e)
def setup_inputs_dry(rng):
    a, m, u, e = parts(rng); z = firsts(e); o = rng.permutation(8)
    a[:, o[1]] = np.where(z[:, o[1]][:, None], rng.integers(100, 256, (N, 15, V)), rng.integers(0, 100, (N, 15, V)))
    for g in (o[3], o[4]):
        a[:, g] = np.where(rng.random((N, 15, V)) < 0.7, 255, rng.integers(0, 101, (N, 15, V)))
    a[:, o[3], :, ::B] = 0
    u[:, o[5]] = aim(rng, e, o[5], cover(rng))
    a[:, o[5]] = np.where(z[:, o[5]][:, None], rng.integers(0, 31, (N, 15, V)), rng.integers(80, 256, (N, 15, V)))
    a[:, o[5], :, ::B] = rng.integers(60, 101, (N, 15, NO))
    m[:, o[0]] = 1; m[:, o[2]] = rng.random((N, V)) < 0.9; m[:, o[3]] = 1; m[:, o[4]] = rng.random((N, V)) < 0.95
    m[:, o[5]] = 1; m[:, o[5], ::B] = 0
    m[(rng.integers(-2, 1) + np.arange(3)) % N] = 1
    return pack(a, m, u, e)
def setup_inputs_spread(rng):
    a, m, u, e = parts(rng); s = np.exp2(8.2 * rng.random((N, 8, 1, V)))
    a = np.minimum((s * rng.random(a.shape)).astype(np.int64), 255); m = (rng.random(m.shape) < rng.random((N, 8, 1)) * 0.5).astype(np.int64)
    return pack(a, m, u, e)
def check_inputs(d):
    bad = []
    r = d["rec"].astype(np.float32).reshape(N, 8, 16, V); a, m = r[:, :, :15], r[:, :, 15]
    if not np.all((a >= 0) & (a <= 255) & (a == np.floor(a))): bad.append("notes in rec")
    if not np.all((m == 0) | (m == 1)): bad.append("marks in rec")
    if np.min(d["up"]) < 0 or np.max(d["up"]) > V - 1: bad.append("range of up")
    u = np.sort(d["up"].reshape(N, 8, 16, NB, B).transpose(0, 1, 3, 2, 4).reshape(N, 8, NB, 16 * B), axis=-1)
    if np.any(u[..., 1:] == u[..., :-1]): bad.append("different parents in a bank of up")
    if np.min(d["fr"]) < 0 or np.max(d["fr"]) > B - 1: bad.append("range of fr")
    e = np.sort(np.stack([gentries(z) for z in d["fr"]]).reshape(N, 8, NO, K), axis=-1)
    if np.any(e[..., 1:] == e[..., :-1]): bad.append("different places in a bank of fr")
    return bad
def reference(rec, up, fr):
    s = rec.astype(np.float32).astype(np.int64).reshape(N, 8, 16, V); a = s[:, :, :15].copy(); mark = s[:, :, 15] > 0
    u = up.astype(np.int64).reshape(N, 8, 16, NB, B)
    e = np.stack([gentries(z) for z in fr]).astype(np.int64).reshape(N, 8, NO, K); live = np.ones(e.shape, bool)
    for wave in range(RO):
        node = e + B * np.arange(NO)[:, None]
        x = np.take_along_axis(a, node.reshape(N, 8, 1, NO * K), 3).reshape(N, 8, 15, NO, K)
        ee, ll, xx = every(e), every(live), every(np.moveaxis(x, 2, 3))
        new = a.copy(); hit = np.zeros((N, 8, V), bool)
        for b in range(NB):
            q = np.take_along_axis(u[:, :, :, b], ee[:, :, None, b], 3).reshape(N, 8, 1, 16 * K)
            old = np.take_along_axis(a, q, 3)
            arr = np.tile(xx[:, :, b], (1, 1, 1, 16))
            ok = (np.add.reduce((old >= arr).astype(np.int64), axis=2) >= TH) & np.tile(ll[:, :, b], (1, 1, 16))
            r, g, j = np.nonzero(ok); to = q[r, g, 0, j]
            new[r, g, :, to] = ((old + arr) >> 1)[r, g, :, j]
            hit[r, g, to] = True
        h = (hit & ~mark).reshape(N, 8, NO, B); mark = mark | hit; a = new
        e = np.argsort(~h, axis=-1, kind="stable")[..., :K]; live = np.take_along_axis(h, e, 3)
    return {"y": np.concatenate([a, mark[:, :, None].astype(np.int64)], axis=2).reshape(N, 128, V).astype(np.float32).astype(BF)}

@@ -1,0 +1,445 @@
+from concourse.bass import DstId, RemoteDMATransfer
+from concourse.mybir import AluOpType, ActivationFunctionType
+
+ALU = AluOpType
+ACT = ActivationFunctionType
+MAGIC = 8388608.0
+SCALE = 0.5 - 1.0 / 4096
+WAVES = 4
+CH = [(0, 2), (2, 4), (4, 6), (6, 8), (8, 12), (12, 16), (16, 20)]
+GR = [[0], [1], [2, 3], [4], [5], [6]]
+ORDER = ("P0 P2 P1 Q0 Q1 D0 S0 f0 f2 D1 Q2 s0 v0 S1 C0 P3 s1 K0 q3 Q5 f1 O0 S2 f3 X0 v1 D2 D3 C1 O1 v2 s2 X1 S3 s3 q4 K1 C2 O2 "
+         "v3 D4 X2 s4 D5 s5 G0 S4 C3 S5 P9 C4 v4 q6 v5 O3 X3 O4 D6 X4 s6 S6 v6 C5 O5 X5")
+SNAP = [("V", 0, 4), ("A", 4, 8), ("V", 8, 11), ("A", 11, 14), ("V", 14, 15), ("A", 15, 16)]
+SLOT = 48
+
+SCRATCH = {
+    "UPW": ("sbuf", [128, 1920], "int32"),
+    "UPG": ("sbuf", [128, 480], "int32"),
+    "Bs": ("sbuf", [128, 2048], "bfloat16"),
+    "F": ("sbuf", [128, 4096], "float32"),
+    "Q": ("sbuf", [128, 2560], "bfloat16"),
+    "SG": ("sbuf", [128, 2560], "bfloat16"),
+    "VV": ("sbuf", [128, 2560], "float32"),
+    "P16": ("sbuf", [128, 160], "uint16"),
+    "Pf": ("sbuf", [128, 160], "float32"),
+    "OFFS": ("sbuf", [128, 160], "uint16"),
+    "LIST": ("sbuf", [128, 8], "uint16"),
+    "LISTC": ("sbuf", [128, 8], "uint16"),
+    "LISTG": ("sbuf", [128, 2], "uint16"),
+    "GL": ("sbuf", [128, 16 * SLOT], "bfloat16"),
+    "GN": ("sbuf", [128, 32], "bfloat16"),
+    "nT": ("sbuf", [128, 128], "bfloat16"),
+    "nTg": ("sbuf", [128, 128], "bfloat16"),
+    "oldT": ("sbuf", [128, 128], "bfloat16"),
+    "FT": ("sbuf", [128, 128], "bfloat16"),
+    "OKB": ("sbuf", [128, 1024], "bfloat16"),
+    "ONE": ("sbuf", [128, 128], "bfloat16"),
+    "ID": ("sbuf", [128, 128], "bfloat16"),
+    "IDN": ("sbuf", [128, 128], "bfloat16"),
+    "DA": ("sbuf", [128, 128], "bfloat16"),
+    "DB": ("sbuf", [128, 128], "bfloat16"),
+    "ID2": ("sbuf", [128, 128], "float32"),
+    "TRI": ("sbuf", [128, 128], "bfloat16"),
+    "B1": ("sbuf", [128, 8], "bfloat16"),
+    "B2": ("sbuf", [128, 8], "bfloat16"),
+    "BW": ("sbuf", [128, 144], "bfloat16"),
+    "SEL": ("sbuf", [128, 8], "bfloat16"),
+    "EI": ("sbuf", [128, 512], "int32"),
+    "EJ": ("sbuf", [128, 512], "int32"),
+    "EN": ("sbuf", [128, 512], "bfloat16"),
+    "EP": ("sbuf", [128, 512], "bfloat16"),
+    "IP": ("sbuf", [128, 1], "int32"),
+    "IT": ("sbuf", [128, 3], "int32"),
+    "COL": ("sbuf", [128, 16], "float32"),
+    "WV": ("sbuf", [128, 16], "float32"),
+    "JB": ("sbuf", [128, 4], "float32"),
+    "RW": ("sbuf", [128, 80], "bfloat16"),
+    "CI": ("sbuf", [128, 18], "int32"),
+    "CL": ("sbuf", [128, 10], "bfloat16"),
+    "CA": ("sbuf", [128, 10], "bfloat16"),
+    "CLf": ("sbuf", [128, 16], "float32"),
+    "CG": ("sbuf", [128, 2], "bfloat16"),
+    "FRI": ("sbuf", [128, 8], "int32"),
+    "FRF": ("sbuf", [128, 8], "float32"),
+    "LF": ("sbuf", [128, 16], "float32"),
+}
+for _w in range(WAVES):
+    SCRATCH["NB%d" % _w] = ("sbuf", [128, 144], "bfloat16")
+for _n in ("D0", "D1", "S0", "S1", "Y0", "Y1", "X0", "X1"):
+    SCRATCH["ps" + _n] = ("psum", [128, 512], "float32")
+SEMAPHORES = (["sv", "sa", "st", "sg", "lrec", "lfr", "lupg", "lsem"] + ["lup%d" % i for i in range(4)]
+              + ["arr%d" % w for w in range(WAVES)] + ["out%d" % i for i in range(8)])
+CSEM = {"V": "sv", "A": "sa", "T": "st", "G": "sg"}
+
+
+def make_tracker(g, T):
+    qs = {"V": g.vector, "A": g.scalar, "T": g.tensor, "G": g, "S": g.sync}
+    known = {q: {} for q in qs}
+    cnt, lw, rd, pa, seq = {}, {}, {}, {}, [0]
+
+    def settle(q, evs):
+        for ev in sorted(evs, key=lambda e: -e[4]):
+            if known[q].get(ev[1], 0) >= ev[2]:
+                continue
+            qs[q].wait_ge(T.sem[ev[1]], ev[2])
+            for s, v in ev[3].items():
+                if known[q].get(s, 0) < v:
+                    known[q][s] = v
+            known[q][ev[1]] = ev[2]
+
+    def op(q, call, R=(), W=(), sem=None, inc=1):
+        tag = q if sem is None else "dma"
+        evs = []
+        for t in list(R) + list(W):
+            if t[:2] == "ps":
+                evs += [e for k, e in pa.get(t, {}).items() if k != tag]
+        for t in R:
+            if t[:2] != "ps":
+                evs += lw.get(t, [])
+        for t in W:
+            if t[:2] != "ps":
+                evs += lw.get(t, []) + list(rd.get(t, {}).values())
+        settle(q, evs)
+        s = CSEM[q] if sem is None else sem
+        r = call(qs[q])
+        for ins in (r if isinstance(r, list) else [r]):
+            ins.then_inc(T.sem[s], inc)
+            cnt[s] = cnt.get(s, 0) + inc
+        seq[0] += 1
+        ev = (tag, s, cnt[s], dict(known[q]), seq[0])
+        for t in list(R) + list(W):
+            if t[:2] == "ps":
+                pa.setdefault(t, {})[tag] = ev
+        for t in R:
+            if t[:2] != "ps":
+                rd.setdefault(t, {})[tag if tag != "dma" else s] = ev
+        for t in W:
+            if t[:2] != "ps":
+                lw[t] = [ev]
+                rd[t] = {}
+
+    def arrive(t, sem, val):
+        seq[0] += 1
+        lw[t] = [("remote", sem, val, {}, seq[0])]
+
+    def ready(q, toks):
+        settle(q, [e for t in toks for e in lw.get(t, [])])
+
+    def finish(extra):
+        for s, v in list(cnt.items()) + extra:
+            if known["G"].get(s, 0) < v:
+                g.wait_ge(T.sem[s], v)
+    return op, arrive, ready, finish
+
+
+def rank_program(g, core, T, topo):
+    rank = T.rank_of(core)
+    if rank is None:
+        return
+    N = len(T.cores)
+    op, arrive, ready, finish = make_tracker(g, T)
+    BK = ["Bs%d" % b for b in range(16)]
+    BS = BK + ["Bsp"]
+    FF = ["Fa", "Fb"]
+    last = len(CH) - 1
+
+    def vts(out, in0, s1, s2, op0, op1, R, W):
+        if op1 is None:
+            op("V", lambda v: v.tensor_scalar(out, in0, s1, None, op0), R, W)
+        else:
+            op("V", lambda v: v.tensor_scalar(out, in0, s1, s2, op0, op1), R, W)
+
+    def vcopy(out, in_, R, W):
+        op("V", lambda v: v.tensor_copy(out, in_), R, W)
+
+    def fill(ap, c, W):
+        op("V", lambda v: v.memset(ap, c), (), W)
+
+    def sel(out, in_, pat, cmp, base, cm, R, W):
+        op("G", lambda q: q.affine_select(out, in_, pat, cmp, 0.0, base, cm), R, W)
+
+    def iota(out, pat, base, cm, W):
+        op("G", lambda q: q.iota(out, pat, base, cm), (), W)
+
+    def iotaf(out, pat, base, cm, W):
+        op("G", lambda q: q.iota(out, pat, base, cm, allow_small_or_imprecise_dtypes=True), (), W)
+
+    def act(out, in_, R, W, scale=1.0, bias=None):
+        if bias is None:
+            f = ACT.Copy if isinstance(scale, float) else ACT.Identity
+            op("A", lambda a: a.activation(out, in_, f, scale=scale), R, W)
+        else:
+            op("A", lambda a: a.activation(out, in_, ACT.Identity, bias=bias, scale=scale), R, W)
+
+    op("S", lambda s: s.dma_start(T.FRI[:, :], T.fr[:, :]), (), ["FRI"], "lfr", 16)
+    op("A", lambda s: s.dma_start(T.Bs[:, 0:1792], T.rec[:, :]), (), BK, "lrec", 16)
+    for i in range(4):
+        op("S", lambda s: s.dma_start(T.UPW[:, 448 * i:448 * i + 448], T.up[:, 448 * i:448 * i + 448]),
+           (), ["UPW%d" % i], "lup%d" % i, 16)
+    op("S", lambda s: [s.dma_start(T.UPG[:, 120 * d:120 * d + 112], T.up[:, 1792 + 112 * d:1904 + 112 * d]) for d in range(4)],
+       (), ["UPG"], "lupg", 16)
+
+    fill(T.ONE[:, :], 1.0, ["ONE"])
+    iota(T.IP[:, :], [[0, 1]], 0, 1, ["IP"])
+    iota(T.CI[:, 0:10], [[224, 10]], 0, 0, ["CI0"])
+    iota(T.CI[:, 10:18], [[0, 4], [224, 2]], 0, 0, ["CI1"])
+    iota(T.EI[:, :], [[1, 32], [0, 16]], 128, -1, ["EI"])
+    sel(T.ID[:, :], T.ONE[:, :], [[-1, 128]], ALU.is_equal, 0, 1, ["ONE"], ["ID"])
+    sel(T.B1[:, :], T.ONE[:, 0:8], [[-16, 8]], ALU.is_ge, 0, 1, ["ONE"], ["B1"])
+    sel(T.B2[:, :], T.B1[:, :], [[16, 8]], ALU.is_ge, 14, -1, ["B1"], ["B2"])
+    sel(T.SEL[:, :], T.ONE[:, 0:8], [[-16, 8]], ALU.is_equal, -15, 1, ["ONE"], ["SEL"])
+    sel(T.TRI[:, :], T.ONE[:, :], [[1, 128]], ALU.is_ge, 0, -1, ["ONE"], ["TRI"])
+    iotaf(T.WV[:, 0:8], [[-224, 8]], 1679, 0, ["WV0"])
+    iotaf(T.WV[:, 8:16], [[-224, 8]], 1800, 0, ["WV1"])
+    iotaf(T.JB[:, :], [[2, 4]], 9, 0, ["JB"])
+    iota(T.UPW[:, 1792:1920], [[0, 8], [16, 16]], 1792, 1, ["UPWp"])
+    for d in range(4):
+        iota(T.UPG[:, 120 * d + 112:120 * d + 120], [[16, 8]], 1792, 1, ["UPGp%d" % d])
+    C = lambda i: T.COL[:, i:i + 1]
+    vts(T.IT[:, 1:2], T.IP[:, :], 3, 1, ALU.logical_shift_right, ALU.bitwise_and, ["IP"], ["IT1"])
+    vts(T.IT[:, 0:1], T.IP[:, :], 15, None, ALU.bitwise_and, None, ["IP"], ["IT0"])
+    vts(C(3), T.IT[:, 1:2], 112.0, None, ALU.mult, None, ["IT1"], ["c3"])
+    vts(C(0), T.IT[:, 0:1], 14.5, None, ALU.is_lt, None, ["IT0"], ["c0"])
+    vts(T.CLf[:, 0:8], T.CI[:, 0:8], C(3), None, ALU.add, None, ["CI0", "c3"], ["CLf0"])
+    vts(T.CLf[:, 8:16], T.CI[:, 10:18], C(3), None, ALU.add, None, ["CI1", "c3"], ["CLf1"])
+    vts(C(1), C(0), -2.0, 2.0, ALU.mult, ALU.add, ["c0"], ["c1"])
+    vts(T.IT[:, 2:3], T.IP[:, :], 2, 1, ALU.logical_shift_right, ALU.bitwise_and, ["IP"], ["IT2"])
+    fill(T.Bs[:, 1792:2048], 0.0, ["Bsp"])
+    vcopy(T.FRF[:, :], T.FRI[:, :], ["FRI"], ["FRF"])
+    op("V", lambda v: v.tensor_tensor(T.LF[:, 0:8], T.FRF[:, :], T.CLf[:, 0:8], ALU.add), ["FRF", "CLf0"], ["LF0"])
+    op("V", lambda v: v.tensor_tensor(T.LF[:, 8:16], T.FRF[:, :], T.CLf[:, 8:16], ALU.add), ["FRF", "CLf1"], ["LF1"])
+    vcopy(T.NB0[:, 14:16], T.FRI[:, 0:2], ["FRI"], ["NBp0"])
+    vcopy(T.LIST[:, :], T.LF[:, 0:8], ["LF0"], ["LIST"])
+    vcopy(T.LISTC[:, :], T.LF[:, 8:16], ["LF1"], ["LISTC"])
+    vts(T.EJ[:, :], T.EI[:, :], 31, None, ALU.bitwise_and, None, ["EI"], ["EJ"])
+    fill(C(8), MAGIC, ["c8"])
+    fill(C(9), 0.5, ["c9"])
+    fill(C(12), 1.0, ["c12"])
+    fill(T.BW[:, :], 0.0, ["BW"])
+    vts(T.EN[:, :], T.EJ[:, :], 0.0, -1.0, ALU.is_equal, ALU.mult, ["EJ"], ["EN"])
+    act(T.IDN[:, :], T.ID[:, :], ["ID", "c0"], ["IDN"], C(0))
+    act(T.ID2[:, :], T.ID[:, :], ["ID"], ["ID2"], 2.0)
+    act(T.BW[:, 15:128:16], T.B2[:, :], ["B2", "BW"], ["BW"], -1.0 / 32)
+    act(T.EP[:, :], T.EN[:, :], ["EN"], ["EP"], -1.0)
+
+    def late_constants():
+        vcopy(C(2), T.IT[:, 1:2], ["IT1"], ["c2"])
+        vts(C(4), T.IT[:, 1:2], 120.0, None, ALU.mult, None, ["IT1"], ["c4"])
+        vts(C(5), T.IT[:, 1:2], -1.0, 1.0, ALU.mult, ALU.add, ["IT1"], ["c5"])
+        vts(C(7), T.IP[:, :], 120.0, None, ALU.is_equal, None, ["IP"], ["c7"])
+        vts(C(10), T.IP[:, :], 120.0, None, ALU.not_equal, None, ["IP"], ["c10"])
+        vcopy(C(11), T.IT[:, 2:3], ["IT2"], ["c11"])
+        fill(C(13), 240.0, ["c13"])
+        fill(T.CL[:, 8:10], 0.0, ["CL1"])
+        fill(T.RW[:, :], 0.0, ["RW"])
+        fill(T.FT[:, :], 1.0, ["FT"])
+        vcopy(T.TRI[:, 120:121], T.TRI[:, 111:112], ["TRI"], ["TRI"])
+
+    def late_scalar():
+        act(T.DA[:, :], T.ID[:, :], ["ID", "c5"], ["DA"], C(5))
+        act(T.DB[:, :], T.ID[:, :], ["ID", "c2"], ["DB"], C(2))
+        act(T.CG[:, 0:1], C(4), ["c4"], ["CG0"])
+        act(T.CG[:, 1:2], C(4), ["c4", "c13"], ["CG1"], 1.0, C(13))
+        act(T.CL[:, 0:8], T.CLf[:, 0:8], ["CLf0"], ["CL0"], 2.0)
+        act(T.CA[:, 0:8], T.WV[:, 8:16], ["WV1", "c11"], ["CA0"], C(11))
+        act(T.CA[:, 8:9], C(11), ["c11"], ["CA1"], 120.0)
+        act(T.CA[:, 9:10], C(11), ["c11"], ["CA2"], 120.0)
+        act(T.RW[:, 0:80:11], T.WV[:, 0:8], ["WV0", "c7", "c12", "RW"], ["RW"], C(7), C(12))
+        act(T.RW[:, 8:9], C(10), ["c10"], ["RW"])
+        act(T.RW[:, 19:20], C(10), ["c10"], ["RW"])
+
+    def marks(lo, hi):
+        op("T", lambda t: [t.matmul(T.psX1[0:112, 16 * (b // 2) + b % 2:16 * (b // 2) + 16:2],
+                                    T.Bs[:, 112 * b:112 * b + 112], T.SEL[:, :], True, True) for b in range(lo, hi)],
+           BK[lo:hi] + ["SEL"], ["psX1"])
+
+    def keep_marks():
+        act(T.oldT[0:112, :], T.psX1[0:112, 0:128], ["psX1"], ["oldT"])
+
+    def gather(q, i):
+        a, b = CH[i]
+        out, win = T.Q[:, 128 * a:128 * b], T.Bs[:, :].indirect(T.P16[:, 8 * a:8 * b])
+        if q == "V":
+            vcopy(out, win, BS + ["P%d" % i], ["Q%d" % i])
+        else:
+            act(out, win, BS + ["P%d" % i], ["Q%d" % i])
+
+    def piece(i, kind="D"):
+        bank = "ps%s%d" % (kind, i % 2)
+        a, b = CH[i]
+        if a < 16:
+            k = a // 4 * 32
+            x = 128 * (a % 4)
+            return 128 * (b - a), bank, T.nT[k:k + 32, :], slice(k, k + 32), slice(x, x + 128 * (b - a)), "nT"
+        return 128 * (b - a), bank, T.nTg[0:32, :], slice(0, 32), slice(0, 512), "nTg"
+
+    def diff(i):
+        n, ps, w, kr, xr, tok = piece(i)
+        a = 128 * CH[i][0]
+        op("T", lambda t: [t.matmul(T[ps][:, 0:n], T.IDN[:, :], T.Q[:, a:a + n], True, False),
+                           t.matmul(T[ps][:, 0:n], w, T.EN[kr, xr], False, True)], ["Q%d" % i, "IDN", "EN", tok], [ps])
+
+    def total(i):
+        n, ps, w, kr, xr, tok = piece(i, "S")
+        a = 128 * CH[i][0]
+        op("T", lambda t: [t.matmul(T[ps][:, 0:n], T.IDN[:, :], T.Q[:, a:a + n], True, False),
+                           t.matmul(T[ps][:, 0:n], w, T.EP[kr, xr], False, True)], ["Q%d" % i, "IDN", "EP", tok], [ps])
+
+    def sign(i):
+        n, ps = piece(i)[:2]
+        a = 128 * CH[i][0]
+        op("A", lambda s: s.activation(T.SG[:, a:a + n], T[ps][:, 0:n], ACT.Sign, bias=C(9)), [ps, "c9"], ["SG%d" % i])
+
+    def value(i):
+        n, ps = piece(i, "S")[:2]
+        a = 128 * CH[i][0]
+        act(T.VV[:, a:a + n], T[ps][:, 0:n], [ps, "c8"], ["VV%d" % i], SCALE, C(8))
+
+    def cols(gi):
+        return 8 * CH[GR[gi][0]][0], 8 * CH[GR[gi][-1]][1], "psY%d" % (gi % 2)
+
+    def count(gi):
+        lo, hi, ps = cols(gi)
+        out = T[ps][:, 0:hi - lo]
+        op("T", lambda t: [t.matmul(out, T.ID2[:, :], T.Pf[:, lo:hi], True, False)], ["ID2"] + ["Pf%d" % i for i in GR[gi]], [ps])
+        op("T", lambda t: [t.matmul(out, T.BW[:, 15 - k:143 - k], T.SG[:, 16 * lo + k:16 * hi:16], False, k == 15) for k in range(16)],
+           ["BW"] + ["SG%d" % i for i in GR[gi]], [ps])
+
+    def offsets(gi):
+        lo, hi, ps = cols(gi)
+        vts(T.OFFS[:, lo:hi], T[ps][:, 0:hi - lo], 0.5625, None, ALU.add, None, [ps], ["OF%d" % gi])
+
+    def scatter(gi):
+        for i in GR[gi]:
+            for b in range(*CH[i]):
+                vts(T.F[:, :].indirect(T.OFFS[:, 8 * b:8 * b + 8]), T.VV[:, 128 * b:128 * b + 128], 1.0, -MAGIC,
+                    ALU.mult, ALU.add, ["OF%d" % gi, "VV%d" % i], FF)
+
+    def pf(i, j):
+        a, b = 8 * CH[i][0], 8 * CH[j][1]
+        vcopy(T.Pf[:, a:b], T.P16[:, a:b], ["P%d" % k for k in range(i, j + 1)], ["Pf%d" % k for k in range(i, j + 1)])
+
+    def send(w):
+        dst = [T.cores[(rank + d) % N] for d in range(1, 5)]
+        common = [e for e in topo.engines(core, dst[0]) if all(e in topo.engines(core, c) for c in dst)]
+        ne = max(x for x in (1, 2, 4, 8, 16) if x <= len(common))
+        m = sum(1 << e for e in common[:ne])
+        ids = []
+        for c in dst:
+            rid, pid = topo.addr(c, core)
+            ids.append(DstId(rid=rid, pnc=pid))
+        ready("G", ["NBn%d" % w, "NBp%d" % w])
+        g.remote_dma_fused([RemoteDMATransfer(
+            dst_ids=ids, dma_engine_mask=m, remote_sem=T.sem["arr%d" % w], srcs=[T["NB%d" % w][:, 14:48]],
+            dsts=[T.GL[:, (4 * w + d) * SLOT:(4 * w + d) * SLOT + 34] for d in range(4)])], local_sem=T.sem["lsem"])
+        arrive("GL%d" % w, "arr%d" % w, 4 * ne)
+        return ne
+
+    def nodes(w):
+        NBt = T["NB%d" % w]
+        act(NBt[:, 16:144], T.Bs[:, :].indirect(T.LIST[:, :]), BS + ["LIST", "c0", "c1"], ["NBn%d" % w], C(0), C(1))
+        op("T", lambda t: [t.matmul(T.psX0[:, 0:128], NBt[:, 16:144], T.ID[:, :], True, True)], ["NBn%d" % w, "ID"], ["psX0"])
+        act(T.nT[:, :], T.psX0[:, 0:128], ["psX0"], ["nT"])
+
+    def ghosts_in(w):
+        for d in range(4):
+            s = (4 * w + d) * SLOT + 2 + 8 * d
+            sel(T.GN[:, 8 * d:8 * d + 8], T.GL[:, s:s + 8], [[0, 8]], ALU.is_gt, 1, 0, ["GL%d" % w], ["GN%d" % d])
+
+    def ghosts_list(w):
+        def mm(t):
+            r = []
+            for x in range(2):
+                o = T.psX1[:, x:x + 1]
+                s = (4 * w + 2 * x) * SLOT + x
+                r += [t.matmul(o, T.ID[:, :], T.CG[:, x:x + 1], True, False), t.matmul(o, T.DA[:, :], T.GL[:, s:s + 1], False, False),
+                      t.matmul(o, T.DB[:, :], T.GL[:, s + SLOT:s + SLOT + 1], False, True)]
+            return r
+        op("T", mm, ["ID", "DA", "DB", "CG0", "CG1", "GL%d" % w], ["psX1"])
+
+    def ghosts_nT():
+        op("T", lambda t: [t.matmul(T.psX0[0:32, 0:128], T.GN[:, :], T.ID[:, :], True, True)],
+           ["ID"] + ["GN%d" % d for d in range(4)], ["psX0"])
+        act(T.nTg[0:32, :], T.psX0[0:32, 0:128], ["psX0"], ["nTg"])
+
+    def ghosts_parents():
+        vcopy(T.LISTG[:, :], T.psX1[:, 0:2], ["psX1"], ["LISTG"])
+        vcopy(T.P16[:, 128:160], T.UPG[:, :].indirect(T.LISTG[:, :]), ["LISTG", "UPG"] + ["UPGp%d" % d for d in range(4)], ["P%d" % last])
+        pf(last, last)
+
+    def snap(q, lo, hi):
+        out, in_ = T.Bs[:, 112 * lo:112 * hi], T.F[:, 224 * lo:224 * hi:2]
+        if q == "V":
+            vcopy(out, in_, FF, BK[lo:hi])
+        else:
+            act(out, in_, FF, BK[lo:hi])
+
+    def frontier(w):
+        op("T", lambda t: [t.matmul(T.psX0[:, 0:10], T.ID[:, :], T.CL[:, :], True, False),
+                           t.matmul(T.psX0[:, 0:10], T.ID[:, :], T.CA[:, :], False, False)],
+           ["ID", "CL0", "CL1", "CA0", "CA1", "CA2"], ["psX0"])
+        for q, lo, hi in SNAP:
+            snap(q, lo, hi)
+        for q, lo, hi in SNAP:
+            marks(lo, hi)
+        op("V", lambda v: v.tensor_tensor(T.FT[0:112, :], T.psX1[0:112, 0:128], T.oldT[0:112, :], ALU.subtract), ["psX1", "oldT"], ["FT"])
+        for ps in ("psY0", "psY1"):
+            op("T", lambda t: [t.matmul(T[ps][0:121, 0:128], T.TRI[0:120, 0:121], T.FT[0:120, :], True, True)], ["TRI", "FT"], [ps])
+        for j in range(4):
+            vts(T.OKB[0:121, j:1024:8], T.psY0[0:121, 0:128], j + 0.5, 2.0, ALU.is_lt, ALU.mult, ["psY0"], ["OK%d" % j])
+            op("A", lambda a: a.activation(T.OKB[0:121, j + 4:1024:8], T.psY1[0:121, 0:128], ACT.Sign, bias=T.JB[0:121, j:j + 1], scale=-2.0),
+               ["psY1", "JB"], ["OK%d" % (j + 4)])
+        keep_marks()
+        op("T", lambda t: [t.matmul(T.psX0[:, 0:10], T.OKB[0:121, 128 * c:128 * c + 128], T.RW[0:121, 10 * c:10 * c + 10], False, c == 7)
+                           for c in range(8)], ["RW"] + ["OK%d" % j for j in range(8)], ["psX0"])
+        vts(T.LIST[:, :], T.psX0[:, 0:8], 0.5, None, ALU.mult, None, ["psX0"], ["LIST"])
+        act(T["NB%d" % (w + 1)][:, 14:16], T.psX0[:, 8:10], ["psX0"], ["NBp%d" % (w + 1)], 0.5)
+
+    def steps(text, w):
+        one = {"Q": lambda n: gather("V", n), "q": lambda n: gather("A", n), "D": diff, "s": sign, "S": total, "v": value,
+               "C": count, "O": offsets, "X": scatter}
+        for t in text.split():
+            n = int(t[1:])
+            if t[0] in one:
+                one[t[0]](n)
+            elif t[0] == "G":
+                ghosts_in(w)
+                ghosts_list(w)
+                ghosts_nT()
+            elif t == "P9":
+                ghosts_parents()
+            elif t[0] in "Pf":
+                ks = [k for k in range(last) if CH[k][0] // 4 == n] if w == 0 else list(range(last))
+                if w and n:
+                    continue
+                if t[0] == "f":
+                    pf(ks[0], ks[-1])
+                elif w == 0:
+                    vcopy(T.P16[:, 32 * n:32 * n + 32], T.UPW[:, 448 * n:448 * n + 448].indirect(T.LISTC[:, 2 * n:2 * n + 2]),
+                          ["LISTC", "UPW%d" % n], ["P%d" % k for k in ks])
+                else:
+                    vcopy(T.P16[:, 0:128], T.UPW[:, :].indirect(T.LIST[:, :]), ["LIST", "UPWp"] + ["UPW%d" % i for i in range(4)],
+                          ["P%d" % k for k in ks])
+            elif w == 0 and t == "K0":
+                vcopy(T.F[:, 0:896:2], T.Bs[:, 0:448], BK[0:4], ["Fa"])
+                late_constants()
+            elif w == 0 and t == "K1":
+                marks(0, 16)
+                keep_marks()
+                late_scalar()
+
+    ne = 0
+    for w in range(WAVES):
+        nodes(w)
+        if w == 0:
+            act(T.F[:, 896:3584:2], T.Bs[:, 448:1792], BK[4:16], ["Fb"])
+        ne = send(w)
+        steps(ORDER, w)
+        if w + 1 < WAVES:
+            frontier(w)
+    for k, (q, lo, hi) in enumerate(SNAP):
+        snap(q, lo, hi)
+        op("S" if q == "V" else "A", lambda s: s.dma_start(T.y[:, 112 * lo:112 * hi], T.Bs[:, 112 * lo:112 * hi]),
+           BK[lo:hi], ["y%d" % k], "out%d" % k, 16)
+    finish([("lsem", ne * WAVES)] + [("arr%d" % w, 4 * ne) for w in range(WAVES)])

@@ -4,60 +4,84 @@ from concourse.mybir import AluOpType, ActivationFunctionType
 ALU = AluOpType
 ACT = ActivationFunctionType
 MAGIC = 8388608.0
-SCALE = 0.5 - 1.0 / 4096
+HALF = 0.5 - 1.0 / 2048
 WAVES = 4
-CH = [(0, 2), (2, 4), (4, 6), (6, 8), (8, 12), (12, 16), (16, 20)]
-GR = [[0], [1], [2, 3], [4], [5], [6]]
-ORDER = ("P0 P2 P1 Q0 Q1 D0 S0 f0 f2 D1 Q2 s0 v0 S1 C0 P3 s1 K0 q3 Q5 f1 O0 S2 f3 X0 v1 D2 D3 C1 O1 v2 s2 X1 S3 s3 q4 K1 C2 O2 "
-         "v3 D4 X2 s4 D5 s5 G0 S4 C3 S5 P9 C4 v4 q6 v5 O3 X3 O4 D6 X4 s6 S6 v6 C5 O5 X5")
-SNAP = [("V", 0, 4), ("A", 4, 8), ("V", 8, 11), ("A", 11, 14), ("V", 14, 15), ("A", 15, 16)]
+ENT, NODE = 32, 192
+NONE = 4096.0
+NA = 8
+CH = [(0, 4, "V", "V"), (4, 8, "A", "V"), (8, 12, "A", "V"), (12, 16, "A", "V"), (16, 20, "A", "V")]
+GR = [[0], [1], [2], [3], [4]]
+FIRST = ("N0 K2 K7 K1 K5 K9 K6 P0 n0 K3 f0 Q0 P1 Q1 E0 E1 s0 P2 f1 f2 Q2 C0 s1 C1 O0 E2 P3 Q3 K4 K8 E3 O1 K0 X0 s2 C2 s3 f3 O2 X8 X1 X2 C3 G0 "
+         "X9 G1 X3 O3 X4 X10 X11 a1 X12 X13 G2 a0 G3 M0 E4 Q4 X5 G4 X14 s4 X6 C4 X7 R0 X15 O4 X16 g0 H0 H1 X17 H2 H3 X18 R1 X19 H4")
+ORDER = ("N0 Q0 f0 n0 E0 Q2 E2 Q1 s0 C0 E1 R0 s2 O0 Q3 s1 X0 C2 O2 E3 C1 X1 M0 X8 s3 O1 X9 G0 X10 G2 C3 G1 X11 R1 O3 a1 a0 X2 X3 X12 G4 G3 "
+         "Q4 X4 X5 E4 X13 s4 X6 X7 C4 H0 H1 g0 X14 H2 X15 H3 H4 O4 X16 X17 X18 X19")
+TAIL = "x0 x1 m0 t0 m1 t1 l0 F0 w0 l1 t2 c0 l2 w2 t3 a2 a3 u0 l3 b0 b2 k0 w3 L0 r2 w1 r0 L1 b1 Z0 b3 r1 S0 r3 p0"
+LAST = "x0 x1 m0 t0 m1 t1 l0 w0 l1 t2 t3 l2 l3 w1 a2 w2 b0 w3 b1 a3 b2 r0 r1 b3 r2 r3"
+RL = "AVAV"
+WQ = "AVAA"
+WL = "AVAV"
+RQ = "VVAA"
+ZQ = UQ = "V"
+GQ = "A"
 SLOT = 48
 
 SCRATCH = {
     "UPW": ("sbuf", [128, 1920], "int32"),
     "UPG": ("sbuf", [128, 480], "int32"),
-    "Bs": ("sbuf", [128, 2048], "bfloat16"),
-    "F": ("sbuf", [128, 4096], "float32"),
+    "B0": ("sbuf", [128, 2240], "bfloat16"),
+    "B1": ("sbuf", [128, 2240], "bfloat16"),
+    "IA0": ("sbuf", [128, 4096], "float32"),
+    "IA1": ("sbuf", [128, 4096], "float32"),
+    "IV0": ("sbuf", [128, 4096], "bfloat16"),
+    "IV1": ("sbuf", [128, 4096], "bfloat16"),
+    "SA": ("sbuf", [128, 2560], "float32"),
+    "SV": ("sbuf", [128, 2560], "bfloat16"),
+    "R0": ("sbuf", [128, 256], "bfloat16"),
     "Q": ("sbuf", [128, 2560], "bfloat16"),
     "SG": ("sbuf", [128, 2560], "bfloat16"),
-    "VV": ("sbuf", [128, 2560], "float32"),
+    "W": ("sbuf", [128, 1792], "float16"),
+    "IDO": ("sbuf", [128, 128], "bfloat16"),
     "P16": ("sbuf", [128, 160], "uint16"),
-    "Pf": ("sbuf", [128, 160], "float32"),
+    "Pf": ("sbuf", [128, 160], "float16"),
     "OFFS": ("sbuf", [128, 160], "uint16"),
-    "LIST": ("sbuf", [128, 8], "uint16"),
+    "LIST": ("sbuf", [128, 10], "uint16"),
     "LISTC": ("sbuf", [128, 8], "uint16"),
     "LISTG": ("sbuf", [128, 2], "uint16"),
+    "L16": ("sbuf", [128, 112], "uint16"),
+    "LA": ("sbuf", [128, 128], "float32"),
+    "LX": ("sbuf", [128, 132, 4], "float16"),
     "GL": ("sbuf", [128, 16 * SLOT], "bfloat16"),
-    "GN": ("sbuf", [128, 32], "bfloat16"),
     "nT": ("sbuf", [128, 128], "bfloat16"),
     "nTg": ("sbuf", [128, 128], "bfloat16"),
-    "oldT": ("sbuf", [128, 128], "bfloat16"),
+    "THR": ("sbuf", [128, 128], "bfloat16"),
     "FT": ("sbuf", [128, 128], "bfloat16"),
-    "OKB": ("sbuf", [128, 1024], "bfloat16"),
-    "ONE": ("sbuf", [128, 128], "bfloat16"),
+    "CUM": ("sbuf", [128, 4, 16, 2], "bfloat16"),
+    "OKB": ("sbuf", [128, 4, 128, 2], "bfloat16"),
+    "ONE": ("sbuf", [128, 528], "bfloat16"),
+    "EG": ("sbuf", [128, 512], "bfloat16"),
     "ID": ("sbuf", [128, 128], "bfloat16"),
-    "IDN": ("sbuf", [128, 128], "bfloat16"),
-    "DA": ("sbuf", [128, 128], "bfloat16"),
-    "DB": ("sbuf", [128, 128], "bfloat16"),
-    "ID2": ("sbuf", [128, 128], "float32"),
+    "IDH": ("sbuf", [128, 128], "float16"),
+    "IDF": ("sbuf", [128, 128], "float16"),
+    "ID2": ("sbuf", [128, 128], "float16"),
+    "IDM": ("sbuf", [128, 128], "bfloat16"),
     "TRI": ("sbuf", [128, 128], "bfloat16"),
-    "B1": ("sbuf", [128, 8], "bfloat16"),
-    "B2": ("sbuf", [128, 8], "bfloat16"),
-    "BW": ("sbuf", [128, 144], "bfloat16"),
+    "CM": ("sbuf", [128, 128], "bfloat16"),
+    "G1": ("sbuf", [128, 8], "bfloat16"),
+    "G2": ("sbuf", [128, 8], "bfloat16"),
+    "BWA": ("sbuf", [128, 144], "bfloat16"),
+    "BWV": ("sbuf", [128, 144], "bfloat16"),
     "SEL": ("sbuf", [128, 8], "bfloat16"),
-    "EI": ("sbuf", [128, 512], "int32"),
-    "EJ": ("sbuf", [128, 512], "int32"),
+    "SELF": ("sbuf", [128, 8], "float32"),
     "EN": ("sbuf", [128, 512], "bfloat16"),
     "EP": ("sbuf", [128, 512], "bfloat16"),
     "IP": ("sbuf", [128, 1], "int32"),
     "IT": ("sbuf", [128, 3], "int32"),
     "COL": ("sbuf", [128, 16], "float32"),
-    "WV": ("sbuf", [128, 16], "float32"),
-    "JB": ("sbuf", [128, 4], "float32"),
-    "RW": ("sbuf", [128, 80], "bfloat16"),
+    "BI": ("sbuf", [128, 20], "float32"),
+    "WV": ("sbuf", [128, 8], "float32"),
+    "RW": ("sbuf", [128, 96], "bfloat16"),
     "CI": ("sbuf", [128, 18], "int32"),
-    "CL": ("sbuf", [128, 10], "bfloat16"),
-    "CA": ("sbuf", [128, 10], "bfloat16"),
+    "CL": ("sbuf", [128, 12], "bfloat16"),
     "CLf": ("sbuf", [128, 16], "float32"),
     "CG": ("sbuf", [128, 2], "bfloat16"),
     "FRI": ("sbuf", [128, 8], "int32"),
@@ -69,7 +93,7 @@ for _w in range(WAVES):
 for _n in ("D0", "D1", "S0", "S1", "Y0", "Y1", "X0", "X1"):
     SCRATCH["ps" + _n] = ("psum", [128, 512], "float32")
 SEMAPHORES = (["sv", "sa", "st", "sg", "lrec", "lfr", "lupg", "lsem"] + ["lup%d" % i for i in range(4)]
-              + ["arr%d" % w for w in range(WAVES)] + ["out%d" % i for i in range(8)])
+              + ["arr%d" % w for w in range(WAVES)] + ["out%d" % i for i in range(4)])
 CSEM = {"V": "sv", "A": "sa", "T": "st", "G": "sg"}
 
 
@@ -139,16 +163,23 @@ def rank_program(g, core, T, topo):
         return
     N = len(T.cores)
     op, arrive, ready, finish = make_tracker(g, T)
-    BK = ["Bs%d" % b for b in range(16)]
-    BS = BK + ["Bsp"]
-    FF = ["Fa", "Fb"]
-    last = len(CH) - 1
+    own = [i for i in range(len(CH)) if CH[i][0] < 16]
+    far = [i for i in range(len(CH)) if CH[i][0] >= 16]
+    tab = lambda w: T["B%d" % (w % 2)]
+    nodes_of = lambda w: ["B%dn%d" % (w % 2, i) for i in range(4)]
+    ents_of = lambda w: ["B%de%d" % (w % 2, i) for i in range(6)]
+    col = lambda c: ENT + 8 * ((c - NA) % 20)
+    lane = lambda b: 2 * (b % 2) + b % 4 // 2
+    turned = lambda b: slice(32 * (b // 4) + lane(b), 32 * (b // 4) + 32, 4)
 
     def vts(out, in0, s1, s2, op0, op1, R, W):
         if op1 is None:
             op("V", lambda v: v.tensor_scalar(out, in0, s1, None, op0), R, W)
         else:
             op("V", lambda v: v.tensor_scalar(out, in0, s1, s2, op0, op1), R, W)
+
+    def vtt(out, in0, in1, o, R, W):
+        op("V", lambda v: v.tensor_tensor(out, in0, in1, o), R, W)
 
     def vcopy(out, in_, R, W):
         op("V", lambda v: v.tensor_copy(out, in_), R, W)
@@ -159,166 +190,221 @@ def rank_program(g, core, T, topo):
     def sel(out, in_, pat, cmp, base, cm, R, W):
         op("G", lambda q: q.affine_select(out, in_, pat, cmp, 0.0, base, cm), R, W)
 
+    def gcopy(out, in_, n, R, W):
+        sel(out, in_, [[0, n]], ALU.is_gt, 1, 0, R, W)
+
     def iota(out, pat, base, cm, W):
         op("G", lambda q: q.iota(out, pat, base, cm), (), W)
 
     def iotaf(out, pat, base, cm, W):
         op("G", lambda q: q.iota(out, pat, base, cm, allow_small_or_imprecise_dtypes=True), (), W)
 
-    def act(out, in_, R, W, scale=1.0, bias=None):
+    def act(out, in_, R, W, scale=1.0, bias=None, f=None):
         if bias is None:
-            f = ACT.Copy if isinstance(scale, float) else ACT.Identity
+            f = f or (ACT.Copy if isinstance(scale, float) else ACT.Identity)
             op("A", lambda a: a.activation(out, in_, f, scale=scale), R, W)
         else:
-            op("A", lambda a: a.activation(out, in_, ACT.Identity, bias=bias, scale=scale), R, W)
+            op("A", lambda a: a.activation(out, in_, f or ACT.Identity, bias=bias, scale=scale), R, W)
+
+    def copy(q, out, in_, R, W):
+        (vcopy if q == "V" else act)(out, in_, R, W)
+
+    def mm(calls, R, W):
+        op("T", lambda t: [t.matmul(*c) for c in calls], R, W)
 
     op("S", lambda s: s.dma_start(T.FRI[:, :], T.fr[:, :]), (), ["FRI"], "lfr", 16)
-    op("A", lambda s: s.dma_start(T.Bs[:, 0:1792], T.rec[:, :]), (), BK, "lrec", 16)
+    op("A", lambda s: s.dma_start(T.B0[:, NODE:NODE + 1792], T.rec[:, :]), (), nodes_of(0), "lrec", 16)
     for i in range(4):
         op("S", lambda s: s.dma_start(T.UPW[:, 448 * i:448 * i + 448], T.up[:, 448 * i:448 * i + 448]),
            (), ["UPW%d" % i], "lup%d" % i, 16)
     op("S", lambda s: [s.dma_start(T.UPG[:, 120 * d:120 * d + 112], T.up[:, 1792 + 112 * d:1904 + 112 * d]) for d in range(4)],
        (), ["UPG"], "lupg", 16)
 
+    C = lambda i: T.COL[:, i:i + 1]
+
+    def places(w, src, tok):
+        vts(T["NB%d" % w][:, 12:14], src, C(5), None, ALU.mult, None, [tok, "c5"], ["NBp%d" % w])
+        vts(T["NB%d" % w][:, 14:16], src, C(2), None, ALU.mult, None, [tok, "c2"], ["NBq%d" % w])
+
     fill(T.ONE[:, :], 1.0, ["ONE"])
     iota(T.IP[:, :], [[0, 1]], 0, 1, ["IP"])
-    iota(T.CI[:, 0:10], [[224, 10]], 0, 0, ["CI0"])
-    iota(T.CI[:, 10:18], [[0, 4], [224, 2]], 0, 0, ["CI1"])
-    iota(T.EI[:, :], [[1, 32], [0, 16]], 128, -1, ["EI"])
-    sel(T.ID[:, :], T.ONE[:, :], [[-1, 128]], ALU.is_equal, 0, 1, ["ONE"], ["ID"])
-    sel(T.B1[:, :], T.ONE[:, 0:8], [[-16, 8]], ALU.is_ge, 0, 1, ["ONE"], ["B1"])
-    sel(T.B2[:, :], T.B1[:, :], [[16, 8]], ALU.is_ge, 14, -1, ["B1"], ["B2"])
-    sel(T.SEL[:, :], T.ONE[:, 0:8], [[-16, 8]], ALU.is_equal, -15, 1, ["ONE"], ["SEL"])
-    sel(T.TRI[:, :], T.ONE[:, :], [[1, 128]], ALU.is_ge, 0, -1, ["ONE"], ["TRI"])
-    iotaf(T.WV[:, 0:8], [[-224, 8]], 1679, 0, ["WV0"])
-    iotaf(T.WV[:, 8:16], [[-224, 8]], 1800, 0, ["WV1"])
-    iotaf(T.JB[:, :], [[2, 4]], 9, 0, ["JB"])
-    iota(T.UPW[:, 1792:1920], [[0, 8], [16, 16]], 1792, 1, ["UPWp"])
-    for d in range(4):
-        iota(T.UPG[:, 120 * d + 112:120 * d + 120], [[16, 8]], 1792, 1, ["UPGp%d" % d])
-    C = lambda i: T.COL[:, i:i + 1]
+    iotaf(T.R0[:, :], [[1, 16], [0, 16]], ENT, 0, ["R0"])
+    iotaf(T.BI[:, :], [[8, 20]], 0, 0, ["BI"])
+    iota(T.CI[:, 0:8], [[224, 8]], 0, 0, ["CI0"])
+    iota(T.CI[:, 8:16], [[0, 4], [224, 2]], 0, 0, ["CI1"])
+    sel(T.ID[:, :], T.ONE[:, 0:128], [[-1, 128]], ALU.is_equal, 0, 1, ["ONE"], ["ID"])
+    sel(T.G1[:, :], T.ONE[:, 0:8], [[-16, 8]], ALU.is_ge, 0, 1, ["ONE"], ["G1"])
+    sel(T.G2[:, :], T.G1[:, :], [[16, 8]], ALU.is_ge, 14, -1, ["G1"], ["G2"])
+    act(T.B1[:, NODE + 1792:2240], T.ONE[:, 0:256], ["ONE"], ["B1z"], 0.0, None, ACT.Silu)
+    for b in range(0, NA, 2):
+        n = 128 * min(2, NA - b)
+        act(T.SA[:, 128 * b:128 * b + n], T.R0[:, 0:n], ["R0", "BI"], ["SA%d" % b], 1.0, T.BI[:, (col(b) - ENT) // 8:(col(b) - ENT) // 8 + 1], ACT.Silu)
     vts(T.IT[:, 1:2], T.IP[:, :], 3, 1, ALU.logical_shift_right, ALU.bitwise_and, ["IP"], ["IT1"])
     vts(T.IT[:, 0:1], T.IP[:, :], 15, None, ALU.bitwise_and, None, ["IP"], ["IT0"])
+    vts(T.IT[:, 2:3], T.IP[:, :], 31, None, ALU.bitwise_and, None, ["IP"], ["IT2"])
     vts(C(3), T.IT[:, 1:2], 112.0, None, ALU.mult, None, ["IT1"], ["c3"])
     vts(C(0), T.IT[:, 0:1], 14.5, None, ALU.is_lt, None, ["IT0"], ["c0"])
-    vts(T.CLf[:, 0:8], T.CI[:, 0:8], C(3), None, ALU.add, None, ["CI0", "c3"], ["CLf0"])
-    vts(T.CLf[:, 8:16], T.CI[:, 10:18], C(3), None, ALU.add, None, ["CI1", "c3"], ["CLf1"])
+    vts(C(4), T.IT[:, 2:3], float(ENT), None, ALU.add, None, ["IT2"], ["c4"])
+    vts(C(6), T.IT[:, 2:3], ENT - 16.0, None, ALU.add, None, ["IT2"], ["c6"])
+    vcopy(C(2), T.IT[:, 1:2], ["IT1"], ["c2"])
+    vts(C(5), T.IT[:, 1:2], -1.0, 1.0, ALU.mult, ALU.add, ["IT1"], ["c5"])
     vts(C(1), C(0), -2.0, 2.0, ALU.mult, ALU.add, ["c0"], ["c1"])
-    vts(T.IT[:, 2:3], T.IP[:, :], 2, 1, ALU.logical_shift_right, ALU.bitwise_and, ["IP"], ["IT2"])
-    fill(T.Bs[:, 1792:2048], 0.0, ["Bsp"])
+    fill(T.B0[:, NODE + 1792:2240], 0.0, ["B0z"])
+    fill(T.BWV[:, :], 0.0, ["BWV"])
+    vts(T.EP[:, 0:256], T.R0[:, :], C(4), None, ALU.is_equal, None, ["R0", "c4"], ["EP0"])
+    vts(T.EP[:, 256:512], T.R0[:, :], C(6), None, ALU.is_equal, None, ["R0", "c6"], ["EP1"])
+    vts(T.CLf[:, 0:8], T.CI[:, 0:8], C(3), None, ALU.add, None, ["CI0", "c3"], ["CLf0"])
+    vts(T.CLf[:, 8:16], T.CI[:, 8:16], C(3), None, ALU.add, None, ["CI1", "c3"], ["CLf1"])
     vcopy(T.FRF[:, :], T.FRI[:, :], ["FRI"], ["FRF"])
-    op("V", lambda v: v.tensor_tensor(T.LF[:, 0:8], T.FRF[:, :], T.CLf[:, 0:8], ALU.add), ["FRF", "CLf0"], ["LF0"])
-    op("V", lambda v: v.tensor_tensor(T.LF[:, 8:16], T.FRF[:, :], T.CLf[:, 8:16], ALU.add), ["FRF", "CLf1"], ["LF1"])
-    vcopy(T.NB0[:, 14:16], T.FRI[:, 0:2], ["FRI"], ["NBp0"])
-    vcopy(T.LIST[:, :], T.LF[:, 0:8], ["LF0"], ["LIST"])
+    vtt(T.LF[:, 0:8], T.FRF[:, :], T.CLf[:, 0:8], ALU.add, ["FRF", "CLf0"], ["LF0"])
+    vtt(T.LF[:, 8:16], T.FRF[:, :], T.CLf[:, 8:16], ALU.add, ["FRF", "CLf1"], ["LF1"])
+    places(0, T.FRF[:, 0:2], "FRF")
+    vcopy(T.LIST[:, 0:8], T.LF[:, 0:8], ["LF0"], ["LIST"])
     vcopy(T.LISTC[:, :], T.LF[:, 8:16], ["LF1"], ["LISTC"])
-    vts(T.EJ[:, :], T.EI[:, :], 31, None, ALU.bitwise_and, None, ["EI"], ["EJ"])
-    fill(C(8), MAGIC, ["c8"])
-    fill(C(9), 0.5, ["c9"])
-    fill(C(12), 1.0, ["c12"])
-    fill(T.BW[:, :], 0.0, ["BW"])
-    vts(T.EN[:, :], T.EJ[:, :], 0.0, -1.0, ALU.is_equal, ALU.mult, ["EJ"], ["EN"])
-    act(T.IDN[:, :], T.ID[:, :], ["ID", "c0"], ["IDN"], C(0))
-    act(T.ID2[:, :], T.ID[:, :], ["ID"], ["ID2"], 2.0)
-    act(T.BW[:, 15:128:16], T.B2[:, :], ["B2", "BW"], ["BW"], -1.0 / 32)
-    act(T.EP[:, :], T.EN[:, :], ["EN"], ["EP"], -1.0)
+    vts(T.ID2[:, :], T.ID[:, :], 2.0, None, ALU.mult, None, ["ID"], ["ID2"])
+    vts(T.BWV[:, 15:128:16], T.G2[:, :], -1.0 / 16, None, ALU.mult, None, ["G2", "BWV"], ["BWV"])
+    if any(c[3] == "A" for c in CH):
+        fill(C(9), 0.5, ["c9"])
+        fill(T.BWA[:, :], 0.0, ["BWA"])
+        vts(T.EN[:, :], T.EP[:, :], -1.0, None, ALU.mult, None, ["EP0", "EP1"], ["EN"])
+        vts(T.BWA[:, 15:128:16], T.G2[:, :], -1.0 / 32, None, ALU.mult, None, ["G2", "BWA"], ["BWA"])
 
-    def late_constants():
-        vcopy(C(2), T.IT[:, 1:2], ["IT1"], ["c2"])
-        vts(C(4), T.IT[:, 1:2], 120.0, None, ALU.mult, None, ["IT1"], ["c4"])
-        vts(C(5), T.IT[:, 1:2], -1.0, 1.0, ALU.mult, ALU.add, ["IT1"], ["c5"])
+    def reset(n, w, lo=0, hi=1792):
+        if n == 0:
+            iotaf(T["IA%d" % (w % 2)][:, 2 * lo:2 * hi:2], [[1, hi - lo]], NODE + lo, 0, ["IA%d" % (w % 2)])
+        else:
+            iotaf(T["IV%d" % (w % 2)][:, 2 * lo:2 * hi:2], [[0, hi - lo]], int(NONE), 0, ["IV%d" % (w % 2)])
+
+    def late_gpsimd():
+        for d in range(4):
+            iota(T.UPG[:, 120 * d + 112:120 * d + 120], [[16, 8]], 1792, 1, ["UPGp%d" % d])
+        sel(T.EG[:, :], T.ONE[:, 0:512], [[40, 4], [1, 8], [0, 16]], ALU.is_equal, 0, -1, ["ONE"], ["EG"])
+        sel(T.SEL[:, :], T.ONE[:, 0:8], [[-16, 8]], ALU.is_equal, -15, 1, ["ONE"], ["SEL"])
+        gcopy(T.SELF[:, :], T.SEL[:, :], 8, ["SEL"], ["SELF"])
+        sel(T.TRI[:, 0:120], T.ONE[:, 0:120], [[1, 120]], ALU.is_ge, 0, -1, ["ONE"], ["TRI0"])
+        sel(T.TRI[:, 120:121], T.ONE[:, 0:1], [[0, 1]], ALU.is_ge, 111, -1, ["ONE"], ["TRI1"])
+        iota(T.UPW[:, 1792:1920], [[0, 8], [16, 16]], 1792, 1, ["UPWp"])
+
+    def vector_values():
+        for b in range(NA, 20, 2):
+            n = 128 * min(2, 20 - b)
+            vts(T.SV[:, 128 * b:128 * b + n], T.R0[:, 0:n], float(col(b) - ENT), None, ALU.add, None, ["R0"], ["SV%d" % b])
+
+    def ghost_constants():
+        vts(T.CG[:, 0:1], T.IT[:, 1:2], 120.0, None, ALU.mult, None, ["IT1"], ["CG0"])
+        vts(T.CG[:, 1:2], T.IT[:, 1:2], 120.0, 240.0, ALU.mult, ALU.add, ["IT1"], ["CG1"])
+
+    def columns():
+        fill(C(11), float(NODE), ["c11"])
+        fill(C(12), 256.0, ["c12"])
+        fill(C(8), -MAGIC, ["c8"])
+        vts(C(13), T.IP[:, :], -MAGIC - 128.0, MAGIC, ALU.mult, ALU.add, ["IP"], ["c13"])
         vts(C(7), T.IP[:, :], 120.0, None, ALU.is_equal, None, ["IP"], ["c7"])
-        vts(C(10), T.IP[:, :], 120.0, None, ALU.not_equal, None, ["IP"], ["c10"])
-        vcopy(C(11), T.IT[:, 2:3], ["IT2"], ["c11"])
-        fill(C(13), 240.0, ["c13"])
-        fill(T.CL[:, 8:10], 0.0, ["CL1"])
+        vts(T.WV[:, :], T.CI[:, 0:8], -1.0, 1679.0, ALU.mult, ALU.add, ["CI0"], ["WV"])
         fill(T.RW[:, :], 0.0, ["RW"])
-        fill(T.FT[:, :], 1.0, ["FT"])
-        vcopy(T.TRI[:, 120:121], T.TRI[:, 111:112], ["TRI"], ["TRI"])
 
     def late_scalar():
-        act(T.DA[:, :], T.ID[:, :], ["ID", "c5"], ["DA"], C(5))
-        act(T.DB[:, :], T.ID[:, :], ["ID", "c2"], ["DB"], C(2))
-        act(T.CG[:, 0:1], C(4), ["c4"], ["CG0"])
-        act(T.CG[:, 1:2], C(4), ["c4", "c13"], ["CG1"], 1.0, C(13))
-        act(T.CL[:, 0:8], T.CLf[:, 0:8], ["CLf0"], ["CL0"], 2.0)
-        act(T.CA[:, 0:8], T.WV[:, 8:16], ["WV1", "c11"], ["CA0"], C(11))
-        act(T.CA[:, 8:9], C(11), ["c11"], ["CA1"], 120.0)
-        act(T.CA[:, 9:10], C(11), ["c11"], ["CA2"], 120.0)
-        act(T.RW[:, 0:80:11], T.WV[:, 0:8], ["WV0", "c7", "c12", "RW"], ["RW"], C(7), C(12))
-        act(T.RW[:, 8:9], C(10), ["c10"], ["RW"])
-        act(T.RW[:, 19:20], C(10), ["c10"], ["RW"])
+        act(T.FT[:, :], T.ONE[:, 0:128], ["ONE"], ["FT"])
+        for p in (0, 1):
+            act(T["B%d" % p][:, 0:ENT], T.ONE[:, 0:ENT], ["ONE"], ["B%dy" % p], 0.0)
+        act(T.CL[:, 0:8], T.CLf[:, 0:8], ["CLf0"], ["CL0"])
+        act(T.CL[:, 8:10], T.CLf[:, 0:2], ["CLf0"], ["CL1"])
+        act(T.CL[:, 10:12], T.ONE[:, 0:2], ["ONE"], ["CL2"], 0.0)
+        act(T.IDM[:, :], T.ID[:, :], ["ID"], ["IDM"], -float(NODE))
+        act(T.IDO[:, :], T.ID[:, :], ["ID"], ["IDO"], 0.5)
+        act(T.CM[0:2, :], T.ONE[0:2, 0:128], ["ONE", "c13"], ["CM"], T.COL[0:2, 13:14])
 
-    def marks(lo, hi):
-        op("T", lambda t: [t.matmul(T.psX1[0:112, 16 * (b // 2) + b % 2:16 * (b // 2) + 16:2],
-                                    T.Bs[:, 112 * b:112 * b + 112], T.SEL[:, :], True, True) for b in range(lo, hi)],
-           BK[lo:hi] + ["SEL"], ["psX1"])
+    def late_vector():
+        vts(T.IDH[:, :], T.ID[:, :], HALF, None, ALU.mult, None, ["ID"], ["IDH"])
+        vcopy(T.IDF[:, :], T.ID[:, :], ["ID"], ["IDF"])
+        vts(T.LX[:, :, :], T.ONE[:, :], 0.0, None, ALU.mult, None, ["ONE"], ["LXz"])
+        vts(T.RW[:, 0:96:13], T.WV[:, :], C(7), 1.0, ALU.mult, ALU.add, ["WV", "c7", "RW"], ["RW"])
+        vts(T.RW[:, 10:24:13], T.ONE[:, 0:2], C(7), None, ALU.subtract, None, ["ONE", "c7", "RW"], ["RW"])
+        vts(T.RW[:, 8:22:13], T.RW[:, 10:24:13], 113.0, -112.0, ALU.mult, ALU.add, ["RW"], ["RW"])
 
-    def keep_marks():
-        act(T.oldT[0:112, :], T.psX1[0:112, 0:128], ["psX1"], ["oldT"])
+    def marks(n, w):
+        if w == 0:
+            mm([(T.psX1[0:112, turned(b)], tab(w)[:, NODE + 112 * b:NODE + 112 * b + 112], T.SEL[:, :], True, True) for b in range(16)],
+               nodes_of(w) + ["SEL"], ["psX1"])
+            act(T.THR[0:112, :], T.psX1[0:112, 0:128], ["psX1", "c11"], ["THR"], -float(NODE), T.COL[0:112, 11:12])
+        elif w + 1 < WAVES:
+            o = T.psX1[0:112, 0:128]
+            mm([(o, T.ID[0:112, 0:112], T.THR[0:112, :], True, False), (o, T.IDM[0:112, 0:112], T.FT[0:112, :], False, True)],
+               ["ID", "IDM", "THR", "FT"], ["psX1"])
+            act(T.THR[0:112, :], o, ["psX1"], ["THR"])
 
-    def gather(q, i):
-        a, b = CH[i]
-        out, win = T.Q[:, 128 * a:128 * b], T.Bs[:, :].indirect(T.P16[:, 8 * a:8 * b])
-        if q == "V":
-            vcopy(out, win, BS + ["P%d" % i], ["Q%d" % i])
+    def gather(i, w):
+        a, b, q = CH[i][:3]
+        copy(q, T.Q[:, 128 * a:128 * b], tab(w)[:, NODE:2240].indirect(T.P16[:, 8 * a:8 * b]),
+             nodes_of(w) + ["B%dz" % (w % 2), "P%d" % i], ["Q%d" % i])
+
+    turn = [0]
+    bank_of = {}
+
+    def spread(i, w):
+        a, b, _, q = CH[i]
+        ps = "psD%d" % (turn[0] % 2)
+        turn[0] += 1
+        bank_of[i] = ps
+        k, x, n = a // 4 * 32, 128 * (a % 4), 128 * (b - a)
+        if a >= 16:
+            mm([(T[ps][:, 0:n], T.nTg[:, :], T.EG[:, x:x + n], True, True)], ["EG", "nTg"], [ps])
+        elif q == "V":
+            mm([(T[ps][:, 0:n], T.nT[k:k + 32, :], T.EP[k:k + 32, x:x + n], True, True)], ["EP0", "EP1", "nT"], [ps])
         else:
-            act(out, win, BS + ["P%d" % i], ["Q%d" % i])
+            mm([(T[ps][:, 0:n], T.nT[k:k + 32, :], T.EN[k:k + 32, x:x + n], True, False), (T[ps][:, 0:n], T.ID[:, :], T.Q[:, 128 * a:128 * b], False, True)],
+               ["Q%d" % i, "ID", "EN", "nT"], [ps])
 
-    def piece(i, kind="D"):
-        bank = "ps%s%d" % (kind, i % 2)
-        a, b = CH[i]
-        if a < 16:
-            k = a // 4 * 32
-            x = 128 * (a % 4)
-            return 128 * (b - a), bank, T.nT[k:k + 32, :], slice(k, k + 32), slice(x, x + 128 * (b - a)), "nT"
-        return 128 * (b - a), bank, T.nTg[0:32, :], slice(0, 32), slice(0, 512), "nTg"
-
-    def diff(i):
-        n, ps, w, kr, xr, tok = piece(i)
-        a = 128 * CH[i][0]
-        op("T", lambda t: [t.matmul(T[ps][:, 0:n], T.IDN[:, :], T.Q[:, a:a + n], True, False),
-                           t.matmul(T[ps][:, 0:n], w, T.EN[kr, xr], False, True)], ["Q%d" % i, "IDN", "EN", tok], [ps])
-
-    def total(i):
-        n, ps, w, kr, xr, tok = piece(i, "S")
-        a = 128 * CH[i][0]
-        op("T", lambda t: [t.matmul(T[ps][:, 0:n], T.IDN[:, :], T.Q[:, a:a + n], True, False),
-                           t.matmul(T[ps][:, 0:n], w, T.EP[kr, xr], False, True)], ["Q%d" % i, "IDN", "EP", tok], [ps])
-
-    def sign(i):
-        n, ps = piece(i)[:2]
-        a = 128 * CH[i][0]
-        op("A", lambda s: s.activation(T.SG[:, a:a + n], T[ps][:, 0:n], ACT.Sign, bias=C(9)), [ps, "c9"], ["SG%d" % i])
-
-    def value(i):
-        n, ps = piece(i, "S")[:2]
-        a = 128 * CH[i][0]
-        act(T.VV[:, a:a + n], T[ps][:, 0:n], [ps, "c8"], ["VV%d" % i], SCALE, C(8))
+    def compare(i, w):
+        a, b, _, q = CH[i]
+        n, ps = 128 * (b - a), bank_of[i]
+        if q == "V":
+            vtt(T.SG[:, 128 * a:128 * b], T.Q[:, 128 * a:128 * b], T[ps][:, 0:n], ALU.is_ge, [ps, "Q%d" % i], ["SG%d" % i])
+        else:
+            act(T.SG[:, 128 * a:128 * b], T[ps][:, 0:n], [ps, "c9"], ["SG%d" % i], 1.0, C(9), ACT.Sign)
 
     def cols(gi):
-        return 8 * CH[GR[gi][0]][0], 8 * CH[GR[gi][-1]][1], "psY%d" % (gi % 2)
+        return 8 * CH[GR[gi][0]][0], 8 * CH[GR[gi][-1]][1], "psY%d" % (gi % 2), CH[GR[gi][0]][3]
 
-    def count(gi):
-        lo, hi, ps = cols(gi)
+    def count(gi, w):
+        lo, hi, ps, q = cols(gi)
         out = T[ps][:, 0:hi - lo]
-        op("T", lambda t: [t.matmul(out, T.ID2[:, :], T.Pf[:, lo:hi], True, False)], ["ID2"] + ["Pf%d" % i for i in GR[gi]], [ps])
-        op("T", lambda t: [t.matmul(out, T.BW[:, 15 - k:143 - k], T.SG[:, 16 * lo + k:16 * hi:16], False, k == 15) for k in range(16)],
-           ["BW"] + ["SG%d" % i for i in GR[gi]], [ps])
+        mm([(out, T.ID2[:, :], T.Pf[:, lo:hi], True, False)]
+           + [(out, T["BW" + q][:, 15 - k:143 - k], T.SG[:, 16 * lo + k:16 * hi:16], False, k == 15) for k in range(16)],
+           ["ID2", "BW" + q] + ["Pf%d" % i for i in GR[gi]] + ["SG%d" % i for i in GR[gi]], [ps])
 
-    def offsets(gi):
-        lo, hi, ps = cols(gi)
-        vts(T.OFFS[:, lo:hi], T[ps][:, 0:hi - lo], 0.5625, None, ALU.add, None, [ps], ["OF%d" % gi])
+    def offsets(gi, w):
+        lo, hi, ps, q = cols(gi)
+        vts(T.OFFS[:, lo:hi], T[ps][:, 0:hi - lo], 0.5625 if q == "A" else 1.03125, None, ALU.add, None, [ps], ["OF%d" % gi])
 
-    def scatter(gi):
-        for i in GR[gi]:
-            for b in range(*CH[i]):
-                vts(T.F[:, :].indirect(T.OFFS[:, 8 * b:8 * b + 8]), T.VV[:, 128 * b:128 * b + 128], 1.0, -MAGIC,
-                    ALU.mult, ALU.add, ["OF%d" % gi, "VV%d" % i], FF)
+    def scatter(b, w):
+        gi = [k for k in range(len(GR)) if cols(k)[0] <= 8 * b < cols(k)[1]][0]
+        off = T.OFFS[:, 8 * b:8 * b + 8]
+        if b < NA:
+            t = "IA%d" % (w % 2)
+            op("A", lambda a: a.activation(T[t][:, :].indirect(off), T.SA[:, 128 * b:128 * b + 128], ACT.Silu),
+               ["OF%d" % gi, "SA%d" % (b // 2 * 2), t], [t])
+        else:
+            t = "IV%d" % (w % 2)
+            vcopy(T[t][:, :].indirect(off), T.SV[:, 128 * b:128 * b + 128], ["OF%d" % gi, "SV%d" % (b - (b - NA) % 2), t], [t])
 
-    def pf(i, j):
-        a, b = 8 * CH[i][0], 8 * CH[j][1]
-        vcopy(T.Pf[:, a:b], T.P16[:, a:b], ["P%d" % k for k in range(i, j + 1)], ["Pf%d" % k for k in range(i, j + 1)])
+    def turn_table(kind, ps, banks, w):
+        t = "I%s%d" % (kind, w % 2)
+        s = "SELF" if kind == "A" else "SEL"
+        mm([(T[ps][0:112, turned(b)], T[t][:, 224 * b:224 * b + 224:2], T[s][:, :], True, True) for b in banks], [t, s], [ps, "T%s%d" % (kind, banks[0])])
+
+    def scalar_table(n, w):
+        if n < 4:
+            turn_table("A", "psX1", range(4 * n, 4 * n + 4), w)
+        else:
+            act(T.LA[0:112, :], T.psX1[0:112, 0:128], ["psX1"] + ["TA%d" % b for b in range(0, 16, 4)], ["LA"])
+
+    def pf(ks):
+        a, b = 8 * CH[ks[0]][0], 8 * CH[ks[-1]][1]
+        vcopy(T.Pf[:, a:b], T.P16[:, a:b], ["P%d" % k for k in ks], ["Pf%d" % k for k in ks])
+
+    def parents():
+        vcopy(T.P16[:, 0:128], T.UPW[:, :].indirect(T.LIST[:, 0:8]), ["LIST", "UPWp"] + ["UPW%d" % i for i in range(4)], ["P%d" % k for k in own])
 
     def send(w):
         dst = [T.cores[(rank + d) % N] for d in range(1, 5)]
@@ -329,117 +415,162 @@ def rank_program(g, core, T, topo):
         for c in dst:
             rid, pid = topo.addr(c, core)
             ids.append(DstId(rid=rid, pnc=pid))
-        ready("G", ["NBn%d" % w, "NBp%d" % w])
+        ready("G", ["NBz%d" % w, "NBp%d" % w, "NBq%d" % w])
         g.remote_dma_fused([RemoteDMATransfer(
-            dst_ids=ids, dma_engine_mask=m, remote_sem=T.sem["arr%d" % w], srcs=[T["NB%d" % w][:, 14:48]],
-            dsts=[T.GL[:, (4 * w + d) * SLOT:(4 * w + d) * SLOT + 34] for d in range(4)])], local_sem=T.sem["lsem"])
+            dst_ids=ids, dma_engine_mask=m, remote_sem=T.sem["arr%d" % w], srcs=[T["NB%d" % w][:, 12:48]],
+            dsts=[T.GL[:, (4 * w + d) * SLOT:(4 * w + d) * SLOT + 36] for d in range(4)])], local_sem=T.sem["lsem"])
         arrive("GL%d" % w, "arr%d" % w, 4 * ne)
-        return ne
+        engines[0] = ne
 
-    def nodes(w):
-        NBt = T["NB%d" % w]
-        act(NBt[:, 16:144], T.Bs[:, :].indirect(T.LIST[:, :]), BS + ["LIST", "c0", "c1"], ["NBn%d" % w], C(0), C(1))
-        op("T", lambda t: [t.matmul(T.psX0[:, 0:128], NBt[:, 16:144], T.ID[:, :], True, True)], ["NBn%d" % w, "ID"], ["psX0"])
+    engines = [0]
+
+    def notes(q, out, win, R, W):
+        if q == "V":
+            vts(out, win, C(0), C(1), ALU.mult, ALU.add, R + ["c0", "c1"], W)
+        else:
+            act(out, win, R + ["c0", "c1"], W, C(0), C(1))
+
+    def sent_notes(w):
+        x = 8 if w else 0
+        notes(ZQ, T["NB%d" % w][:, 16:48], tab(w)[:, NODE:NODE + 448].indirect(T.LIST[:, x:x + 2]), nodes_of(w)[:1] + ["LIST"], ["NBz%d" % w])
+
+    def entries(n, w):
+        notes("A", T["NB%d" % w][:, 48:144], tab(w)[:, NODE:2240].indirect(T.LIST[:, 2:8]), nodes_of(w) + ["B%dz" % (w % 2), "LIST"], ["NBn%d" % w])
+
+    def entries_turned(n, w):
+        mm([(T.psX0[:, 0:128], T["NB%d" % w][:, 16:144], T.ID[:, :], True, True)], ["NBn%d" % w, "NBz%d" % w, "ID"], ["psX0"])
         act(T.nT[:, :], T.psX0[:, 0:128], ["psX0"], ["nT"])
 
-    def ghosts_in(w):
-        for d in range(4):
-            s = (4 * w + d) * SLOT + 2 + 8 * d
-            sel(T.GN[:, 8 * d:8 * d + 8], T.GL[:, s:s + 8], [[0, 8]], ALU.is_gt, 1, 0, ["GL%d" % w], ["GN%d" % d])
-
-    def ghosts_list(w):
-        def mm(t):
-            r = []
+    def ghosts(n, w):
+        s0 = 4 * w * SLOT
+        if n == 0:
             for x in range(2):
-                o = T.psX1[:, x:x + 1]
-                s = (4 * w + 2 * x) * SLOT + x
-                r += [t.matmul(o, T.ID[:, :], T.CG[:, x:x + 1], True, False), t.matmul(o, T.DA[:, :], T.GL[:, s:s + 1], False, False),
-                      t.matmul(o, T.DB[:, :], T.GL[:, s + SLOT:s + SLOT + 1], False, True)]
-            return r
-        op("T", mm, ["ID", "DA", "DB", "CG0", "CG1", "GL%d" % w], ["psX1"])
-
-    def ghosts_nT():
-        op("T", lambda t: [t.matmul(T.psX0[0:32, 0:128], T.GN[:, :], T.ID[:, :], True, True)],
-           ["ID"] + ["GN%d" % d for d in range(4)], ["psX0"])
-        act(T.nTg[0:32, :], T.psX0[0:32, 0:128], ["psX0"], ["nTg"])
-
-    def ghosts_parents():
-        vcopy(T.LISTG[:, :], T.psX1[:, 0:2], ["psX1"], ["LISTG"])
-        vcopy(T.P16[:, 128:160], T.UPG[:, :].indirect(T.LISTG[:, :]), ["LISTG", "UPG"] + ["UPGp%d" % d for d in range(4)], ["P%d" % last])
-        pf(last, last)
-
-    def snap(q, lo, hi):
-        out, in_ = T.Bs[:, 112 * lo:112 * hi], T.F[:, 224 * lo:224 * hi:2]
-        if q == "V":
-            vcopy(out, in_, FF, BK[lo:hi])
+                s = s0 + 2 * x * SLOT + x
+                vts(T.LISTG[:, x:x + 1], T.GL[:, s:s + 1], T.GL[:, s + SLOT + 2:s + SLOT + 3], T.CG[:, x:x + 1], ALU.add, ALU.add,
+                    ["CG%d" % x, "GL%d" % w], ["LISTG%d" % x])
+        elif n == 1:
+            vcopy(T.P16[:, 128:160], T.UPG[:, :].indirect(T.LISTG[:, :]), ["LISTG0", "LISTG1", "UPG"] + ["UPGp%d" % d for d in range(4)],
+                  ["P%d" % k for k in far])
+        elif n == 2:
+            mm([(T.psX0[32 * d:32 * d + 32, 0:128], T.GL[:, s0 + d * SLOT + 4:s0 + d * SLOT + 36], T.ID[:, :], True, True) for d in range(4)],
+               ["ID", "GL%d" % w], ["psX0"])
+        elif n == 3:
+            copy(GQ, T.nTg[:, :], T.psX0[:, 0:128], ["psX0"], ["nTg"])
         else:
-            act(out, in_, FF, BK[lo:hi])
+            pf(far)
 
-    def frontier(w):
-        op("T", lambda t: [t.matmul(T.psX0[:, 0:10], T.ID[:, :], T.CL[:, :], True, False),
-                           t.matmul(T.psX0[:, 0:10], T.ID[:, :], T.CA[:, :], False, False)],
-           ["ID", "CL0", "CL1", "CA0", "CA1", "CA2"], ["psX0"])
-        for q, lo, hi in SNAP:
-            snap(q, lo, hi)
-        for q, lo, hi in SNAP:
-            marks(lo, hi)
-        op("V", lambda v: v.tensor_tensor(T.FT[0:112, :], T.psX1[0:112, 0:128], T.oldT[0:112, :], ALU.subtract), ["psX1", "oldT"], ["FT"])
-        for ps in ("psY0", "psY1"):
-            op("T", lambda t: [t.matmul(T[ps][0:121, 0:128], T.TRI[0:120, 0:121], T.FT[0:120, :], True, True)], ["TRI", "FT"], [ps])
-        for j in range(4):
-            vts(T.OKB[0:121, j:1024:8], T.psY0[0:121, 0:128], j + 0.5, 2.0, ALU.is_lt, ALU.mult, ["psY0"], ["OK%d" % j])
-            op("A", lambda a: a.activation(T.OKB[0:121, j + 4:1024:8], T.psY1[0:121, 0:128], ACT.Sign, bias=T.JB[0:121, j:j + 1], scale=-2.0),
-               ["psY1", "JB"], ["OK%d" % (j + 4)])
-        keep_marks()
-        op("T", lambda t: [t.matmul(T.psX0[:, 0:10], T.OKB[0:121, 128 * c:128 * c + 128], T.RW[0:121, 10 * c:10 * c + 10], False, c == 7)
-                           for c in range(8)], ["RW"] + ["OK%d" % j for j in range(8)], ["psX0"])
-        vts(T.LIST[:, :], T.psX0[:, 0:8], 0.5, None, ALU.mult, None, ["psX0"], ["LIST"])
-        act(T["NB%d" % (w + 1)][:, 14:16], T.psX0[:, 8:10], ["psX0"], ["NBp%d" % (w + 1)], 0.5)
+    def into_table(n, w):
+        e, NBt = ents_of(w), T["NB%d" % w]
+        gcopy(tab(w)[:, col(NA):col(16)], NBt[:, 16 + 8 * NA:144], 128 - 8 * NA, ["NBn%d" % w, "NBz%d" % w], [e[4]])
+        gcopy(tab(w)[:, col(0):col(0) + 8 * NA], NBt[:, 16:16 + 8 * NA], 8 * NA, ["NBn%d" % w, "NBz%d" % w], [e[5]])
+        for d in range(4):
+            s = (4 * w + d) * SLOT + 4 + 8 * d
+            gcopy(tab(w)[:, col(16 + d):col(16 + d) + 8], T.GL[:, s:s + 8], 8, ["GL%d" % w], [e[d]])
 
-    def steps(text, w):
-        one = {"Q": lambda n: gather("V", n), "q": lambda n: gather("A", n), "D": diff, "s": sign, "S": total, "v": value,
-               "C": count, "O": offsets, "X": scatter}
-        for t in text.split():
-            n = int(t[1:])
-            if t[0] in one:
-                one[t[0]](n)
-            elif t[0] == "G":
-                ghosts_in(w)
-                ghosts_list(w)
-                ghosts_nT()
-            elif t == "P9":
-                ghosts_parents()
-            elif t[0] in "Pf":
-                ks = [k for k in range(last) if CH[k][0] // 4 == n] if w == 0 else list(range(last))
-                if w and n:
-                    continue
-                if t[0] == "f":
-                    pf(ks[0], ks[-1])
-                elif w == 0:
-                    vcopy(T.P16[:, 32 * n:32 * n + 32], T.UPW[:, 448 * n:448 * n + 448].indirect(T.LISTC[:, 2 * n:2 * n + 2]),
-                          ["LISTC", "UPW%d" % n], ["P%d" % k for k in ks])
-                else:
-                    vcopy(T.P16[:, 0:128], T.UPW[:, :].indirect(T.LIST[:, :]), ["LIST", "UPWp"] + ["UPW%d" % i for i in range(4)],
-                          ["P%d" % k for k in ks])
-            elif w == 0 and t == "K0":
-                vcopy(T.F[:, 0:896:2], T.Bs[:, 0:448], BK[0:4], ["Fa"])
-                late_constants()
-            elif w == 0 and t == "K1":
-                marks(0, 16)
-                keep_marks()
-                late_scalar()
+    SUM = ["psS0", "psS1", "psD0", "psD1"]
 
-    ne = 0
+    rounder = lambda i, w: (RQ if w + 1 < WAVES else RL)[i]
+    LEAST = ["psX0", "psY0"]
+    TURN = ["psY1", "psX1"]
+
+    def turn_list(i, w):
+        ps = TURN[i % 2]
+        mm([(T[ps][:, 0:28], T.LX[0:112, 32 * i + 3 - r:32 * i + 35 - r, :], T.IDF[0:112, r:112:4], r == 0, r == 3) for r in range(4)],
+           ["LX%d" % (i // 2), "IDF"], [ps])
+
+    def winners(i, w):
+        out, win = T.W[:, 448 * i:448 * i + 448], tab(w)[:, 0:NODE + 1792].indirect(T.L16[:, 28 * i:28 * i + 28])
+        R = nodes_of(w) + ents_of(w) + ["B%dy" % (w % 2), "L16%d" % i]
+        if (WQ if w + 1 < WAVES else WL)[i] == "V":
+            vts(out, win, 256.0, None, ALU.add, None, R, ["W%d" % i])
+        else:
+            act(out, win, R + ["c12"], ["W%d" % i], 1.0, C(12))
+
+    def old_half(i, w):
+        o = T[SUM[i]][:, 0:448]
+        mm([(o, T.CM[0:2, :], T.ONE[0:2, 0:448], True, False)] * (rounder(i, w) == "A")
+           + [(o, T.IDO[:, :], tab(w)[:, NODE + 448 * i:NODE + 448 * i + 448], rounder(i, w) == "V", False)], ["IDO", "CM", "ONE", nodes_of(w)[i]], [SUM[i]])
+
+    def new_half(i, w):
+        ps = T[SUM[i]]
+        mm([(ps[:, 112 * j:112 * j + 112], T.IDH[:, :], T.W[:, 448 * i + lane(j):448 * i + 448:4], False, j == 3) for j in range(4)],
+           ["IDH", SUM[i], "W%d" % i], [SUM[i]])
+
+    def round_down(i, w):
+        out, tok = tab(w + 1)[:, NODE + 448 * i:NODE + 448 * i + 448], nodes_of(w + 1)[i]
+        if rounder(i, w) == "V":
+            vts(out, T[SUM[i]][:, 0:448], MAGIC - 128.0, -MAGIC, ALU.add, ALU.add, [SUM[i]], [tok])
+        else:
+            act(out, T[SUM[i]][:, 0:448], [SUM[i], "c8"], [tok], 1.0, C(8))
+        if w + 1 == WAVES:
+            op("S", lambda s: s.dma_start(T.y[:, 448 * i:448 * i + 448], out), [tok], ["y%d" % i], "out%d" % i, 16)
+
+    def tail(t, w):
+        k, n = t[0], int(t[1:])
+        if k == "x":
+            turn_table("V", LEAST[n], range(8 * n, 8 * n + 8), w)
+        elif k == "m":
+            vtt(T.LX[0:112, 64 * n + 3:64 * n + 67:4, :], T[LEAST[n]][0:112, 64 * n:64 * n + 64], T.LA[0:112, 64 * n:64 * n + 64], ALU.min,
+                [LEAST[n], "LA", "LXz"], ["LX%d" % n])
+        elif k == "t":
+            turn_list(n, w)
+        elif k == "l":
+            vcopy(T.L16[:, 28 * n:28 * n + 28], T[TURN[n % 2]][:, 0:28], [TURN[n % 2]], ["L16%d" % n])
+        elif k == "w":
+            winners(n, w)
+        elif k == "a":
+            old_half(n, w)
+        elif k == "b":
+            new_half(n, w)
+        elif k == "r":
+            round_down(n, w)
+        elif w + 1 == WAVES:
+            return
+        elif k == "F":
+            vtt(T.FT[0:112, :], T.LX[0:112, 3:131:4, :], T.THR[0:112, :], ALU.is_lt, ["LX0", "LX1", "THR"], ["FT"])
+        elif k == "c":
+            mm([(T.psY0[0:121, 0:128], T.TRI[0:120, 0:121], T.FT[0:120, :], True, True)], ["TRI0", "TRI1", "FT"], ["psY0"])
+        elif k == "u":
+            copy(UQ, T.CUM[0:121, :, :, :], T.psY0[0:121, 0:128], ["psY0"], ["CUM"])
+        elif k == "k":
+            for j in range(8):
+                vts(T.OKB[0:121, :, j:128:8, :], T.CUM[0:121, :, :, :], j + 0.5, None, ALU.is_lt, None, ["CUM"], ["OK%d" % j])
+        elif t == "L0":
+            mm([(T.psX0[:, 0:12], T.ID[:, :], T.CL[:, :], True, False)]
+               + [(T.psX0[:, 0:12], T.OKB[0:121, c // 2, :, c % 2], T.RW[0:121, 12 * c:12 * c + 12], False, c == 7) for c in range(8)],
+               ["ID", "CL0", "CL1", "CL2", "RW"] + ["OK%d" % j for j in range(8)], ["psX0"])
+        elif t == "L1":
+            vcopy(T.LIST[:, :], T.psX0[:, 0:10], ["psX0"], ["LIST"])
+            places(w + 1, T.psX0[:, 10:12], "psX0")
+        elif k == "p":
+            parents()
+        elif k == "Z":
+            sent_notes(w + 1)
+        elif k == "S":
+            send(w + 1)
+
+    def step(t, w):
+        one = {"Q": gather, "E": spread, "s": compare, "C": count, "O": offsets, "X": scatter, "a": old_half, "G": ghosts, "g": into_table,
+               "M": marks, "H": scalar_table, "N": entries, "n": entries_turned}
+        k, n = t[0], int(t[1:])
+        if k in one:
+            one[k](n, w)
+        elif k == "R":
+            if w + 1 < WAVES:
+                reset(n, w + 1)
+        elif k == "f":
+            if w == 0 or n == 0:
+                pf([i for i in own if CH[i][0] // 4 == n] if w == 0 else own)
+        elif w == 0 and k == "K":
+            [late_gpsimd, vector_values, ghost_constants, late_scalar, late_vector, columns, lambda: fill(T.IV0[:, 0:3584:2], NONE, ["IV0"]),
+             lambda: reset(0, 0, 0, 896), lambda: reset(0, 0, 896, 1792), lambda: (sent_notes(0), send(0))][n]()
+        elif w == 0 and k == "P":
+            vcopy(T.P16[:, 32 * n:32 * n + 32], T.UPW[:, 448 * n:448 * n + 448].indirect(T.LISTC[:, 2 * n:2 * n + 2]),
+                  ["LISTC", "UPW%d" % n], ["P%d" % i for i in own if CH[i][0] // 4 == n])
+
     for w in range(WAVES):
-        nodes(w)
-        if w == 0:
-            act(T.F[:, 896:3584:2], T.Bs[:, 448:1792], BK[4:16], ["Fb"])
-        ne = send(w)
-        steps(ORDER, w)
-        if w + 1 < WAVES:
-            frontier(w)
-    for k, (q, lo, hi) in enumerate(SNAP):
-        snap(q, lo, hi)
-        op("S" if q == "V" else "A", lambda s: s.dma_start(T.y[:, 112 * lo:112 * hi], T.Bs[:, 112 * lo:112 * hi]),
-           BK[lo:hi], ["y%d" % k], "out%d" % k, 16)
-    finish([("lsem", ne * WAVES)] + [("arr%d" % w, 4 * ne) for w in range(WAVES)])
+        for t in (ORDER if w else FIRST).split():
+            step(t, w)
+        for t in (TAIL if w + 1 < WAVES else LAST).split():
+            tail(t, w)
+    finish([("lsem", engines[0] * WAVES)] + [("arr%d" % w, 4 * engines[0]) for w in range(WAVES)])

@@ -8,22 +8,24 @@ HALF = 0.5 - 1.0 / 2048
 WAVES = 4
 ENT, NODE = 32, 192
 NONE = 4096.0
-NA = 8
-CH = [(0, 4, "V", "V"), (4, 8, "A", "V"), (8, 12, "A", "V"), (12, 16, "A", "V"), (16, 20, "A", "V")]
-GR = [[0], [1], [2], [3], [4]]
-FIRST = ("N0 K2 K7 K1 K5 K9 K6 P0 n0 K3 f0 Q0 P1 Q1 E0 E1 s0 P2 f1 f2 Q2 C0 s1 C1 O0 E2 P3 Q3 K4 K8 E3 O1 K0 X0 s2 C2 s3 f3 O2 X8 X1 X2 C3 G0 "
-         "X9 G1 X3 O3 X4 X10 X11 a1 X12 X13 G2 a0 G3 M0 E4 Q4 X5 G4 X14 s4 X6 C4 X7 R0 X15 O4 X16 g0 H0 H1 X17 H2 H3 X18 R1 X19 H4")
-ORDER = ("N0 Q0 f0 n0 E0 Q2 E2 Q1 s0 C0 E1 R0 s2 O0 Q3 s1 X0 C2 O2 E3 C1 X1 M0 X8 s3 O1 X9 G0 X10 G2 C3 G1 X11 R1 O3 a1 a0 X2 X3 X12 G4 G3 "
-         "Q4 X4 X5 E4 X13 s4 X6 X7 C4 H0 H1 g0 X14 H2 X15 H3 H4 O4 X16 X17 X18 X19")
-TAIL = "x0 x1 m0 t0 m1 t1 l0 F0 w0 l1 t2 c0 l2 w2 t3 a2 a3 u0 l3 b0 b2 k0 w3 L0 r2 w1 r0 L1 b1 Z0 b3 r1 S0 r3 p0"
-LAST = "x0 x1 m0 t0 m1 t1 l0 w0 l1 t2 t3 l2 l3 w1 a2 w2 b0 w3 b1 a3 b2 r0 r1 b3 r2 r3"
-RL = "AVAV"
-WQ = "AVAA"
-WL = "AVAV"
-RQ = "VVAA"
-ZQ = UQ = "V"
-GQ = "A"
-SLOT = 48
+STEP = 64
+NA = 9
+PIECES = [(32 * i, 32 * i + 32) for i in range(5)]
+GATHER = "VAAAA"
+GATHER0 = "AAAAA"
+DBANK = ["D0", "D1", "S0", "S1", "D0"]
+CBANK = ["Y0", "Y1", "Y0", "Y1", "Y0"]
+NARROW = (3,)
+FILL = 640
+FIRST = ("K4 K7 K2 K0 K1 K11 N0 e2 e1 e0 K8 K12 P0 Q0 K9 K10 K3 K6 P1 f1 Q1 P2 s0 Q2 f0 C0 e3 s1 C1 f2 P3 Q3 O0 X0 X1 X2 s2 C2 M0 X3 f3 s3 O2 O1 X9 X10 "
+         "a1 G0 K13 G1 G2 C3 a0 e4 a3 M1 X11 O3 G3 X12 Q4 s4 C4 X4 X5 X6 X7 X8 a2 H0 H1 H2 h3 H3 X13 X14 O4 X15 X16 X17 X18 X19 H4 K5 R0 i0")
+ORDER = ("N0 f0 e2 e1 Q0 s0 C0 Q2 s2 C2 e3 Q1 s1 C1 Q3 O0 R0 i0 X0 X1 X2 X3 O2 X9 G0 s3 C3 a3 G1 X10 G2 Q4 X11 O3 O1 X4 X12 G3 X13 M1 a0 e4 s4 C4 a1 a2 "
+         "X5 X6 X7 X8 H0 H1 H2 h3 H3 X14 X15 O4 X16 X17 X18 X19 H4")
+TAIL = "x0 x1 m0 t0 t1 m1 t2 t3 F0 c0 l0 w0 b0 u0 l1 w2 w1 b1 b2 k0 L0 w3 b3 r0 r2 L1 L2 Z0 S0 e0 r1 p0 r3"
+LAST = "x0 x1 m0 t0 t1 m1 t2 l0 w0 t3 l1 w3 w2 b0 w1 b3 r3 r0 b2 r2 b1 r1"
+WQ, RQ = "AVAA", "VVAA"
+WL, RL = "AVAV", "AVAV"
+SLOT, MID = 64, 28
 
 SCRATCH = {
     "UPW": ("sbuf", [128, 1920], "int32"),
@@ -32,15 +34,15 @@ SCRATCH = {
     "B1": ("sbuf", [128, 2240], "bfloat16"),
     "IA0": ("sbuf", [128, 4096], "float32"),
     "IA1": ("sbuf", [128, 4096], "float32"),
-    "IV0": ("sbuf", [128, 4096], "bfloat16"),
-    "IV1": ("sbuf", [128, 4096], "bfloat16"),
+    "IV": ("sbuf", [128, 4096], "bfloat16"),
+    "IH": ("sbuf", [128, 1792], "float16"),
     "SA": ("sbuf", [128, 2560], "float32"),
     "SV": ("sbuf", [128, 2560], "bfloat16"),
+    "SC": ("sbuf", [128, 512], "bfloat16"),
     "R0": ("sbuf", [128, 256], "bfloat16"),
     "Q": ("sbuf", [128, 2560], "bfloat16"),
     "SG": ("sbuf", [128, 2560], "bfloat16"),
     "W": ("sbuf", [128, 1792], "float16"),
-    "IDO": ("sbuf", [128, 128], "bfloat16"),
     "P16": ("sbuf", [128, 160], "uint16"),
     "Pf": ("sbuf", [128, 160], "float16"),
     "OFFS": ("sbuf", [128, 160], "uint16"),
@@ -50,32 +52,33 @@ SCRATCH = {
     "L16": ("sbuf", [128, 112], "uint16"),
     "LA": ("sbuf", [128, 128], "float32"),
     "LX": ("sbuf", [128, 132, 4], "float16"),
-    "GL": ("sbuf", [128, 16 * SLOT], "bfloat16"),
-    "nT": ("sbuf", [128, 128], "bfloat16"),
-    "nTg": ("sbuf", [128, 128], "bfloat16"),
+    "GL": ("sbuf", [128, 16, SLOT], "bfloat16"),
     "THR": ("sbuf", [128, 128], "bfloat16"),
-    "FT": ("sbuf", [128, 128], "bfloat16"),
+    "FT0": ("sbuf", [128, 128], "bfloat16"),
+    "FT1": ("sbuf", [128, 128], "bfloat16"),
+    "FT2": ("sbuf", [128, 128], "bfloat16"),
     "CUM": ("sbuf", [128, 4, 16, 2], "bfloat16"),
     "OKB": ("sbuf", [128, 4, 128, 2], "bfloat16"),
     "ONE": ("sbuf", [128, 528], "bfloat16"),
-    "EG": ("sbuf", [128, 512], "bfloat16"),
     "ID": ("sbuf", [128, 128], "bfloat16"),
-    "IDH": ("sbuf", [128, 128], "float16"),
     "IDF": ("sbuf", [128, 128], "float16"),
+    "IDH": ("sbuf", [128, 128], "float16"),
+    "IDO": ("sbuf", [128, 128], "bfloat16"),
     "ID2": ("sbuf", [128, 128], "float16"),
     "IDM": ("sbuf", [128, 128], "bfloat16"),
+    "IDL": ("sbuf", [128, 128], "bfloat16"),
+    "IDU": ("sbuf", [128, 128], "bfloat16"),
     "TRI": ("sbuf", [128, 128], "bfloat16"),
+    "UPR": ("sbuf", [128, 128], "bfloat16"),
     "CM": ("sbuf", [128, 128], "bfloat16"),
     "G1": ("sbuf", [128, 8], "bfloat16"),
     "G2": ("sbuf", [128, 8], "bfloat16"),
-    "BWA": ("sbuf", [128, 144], "bfloat16"),
     "BWV": ("sbuf", [128, 144], "bfloat16"),
-    "SEL": ("sbuf", [128, 8], "bfloat16"),
+    "SEL": ("sbuf", [128, 32], "bfloat16"),
     "SELF": ("sbuf", [128, 8], "float32"),
-    "EN": ("sbuf", [128, 512], "bfloat16"),
-    "EP": ("sbuf", [128, 512], "bfloat16"),
+    "SELH": ("sbuf", [128, 8], "float16"),
     "IP": ("sbuf", [128, 1], "int32"),
-    "IT": ("sbuf", [128, 3], "int32"),
+    "IT": ("sbuf", [128, 2], "int32"),
     "COL": ("sbuf", [128, 16], "float32"),
     "BI": ("sbuf", [128, 20], "float32"),
     "WV": ("sbuf", [128, 8], "float32"),
@@ -163,14 +166,15 @@ def rank_program(g, core, T, topo):
         return
     N = len(T.cores)
     op, arrive, ready, finish = make_tracker(g, T)
-    own = [i for i in range(len(CH)) if CH[i][0] < 16]
-    far = [i for i in range(len(CH)) if CH[i][0] >= 16]
-    tab = lambda w: T["B%d" % (w % 2)]
-    nodes_of = lambda w: ["B%dn%d" % (w % 2, i) for i in range(4)]
-    ents_of = lambda w: ["B%de%d" % (w % 2, i) for i in range(6)]
-    col = lambda c: ENT + 8 * ((c - NA) % 20)
+    name = lambda w: "B%d" % (w % 2)
+    tab = lambda w: T[name(w)]
+    nodes_of = lambda w: ["%sn%d" % (name(w), i) for i in range(4)]
+    ents_of = lambda w: ["%se%d" % (name(w), i) for i in range(2)]
+    nodes = lambda w, i: tab(w)[:, NODE + 448 * i:NODE + 448 * i + 448]
+    col = lambda c: NODE - 1 - 8 * c
     lane = lambda b: 2 * (b % 2) + b % 4 // 2
     turned = lambda b: slice(32 * (b // 4) + lane(b), 32 * (b // 4) + 32, 4)
+    last = lambda w: w + 1 == WAVES
 
     def vts(out, in0, s1, s2, op0, op1, R, W):
         if op1 is None:
@@ -201,8 +205,7 @@ def rank_program(g, core, T, topo):
 
     def act(out, in_, R, W, scale=1.0, bias=None, f=None):
         if bias is None:
-            f = f or (ACT.Copy if isinstance(scale, float) else ACT.Identity)
-            op("A", lambda a: a.activation(out, in_, f, scale=scale), R, W)
+            op("A", lambda a: a.activation(out, in_, f or ACT.Copy, scale=scale), R, W)
         else:
             op("A", lambda a: a.activation(out, in_, f or ACT.Identity, bias=bias, scale=scale), R, W)
 
@@ -222,189 +225,187 @@ def rank_program(g, core, T, topo):
 
     C = lambda i: T.COL[:, i:i + 1]
 
-    def places(w, src, tok):
-        vts(T["NB%d" % w][:, 12:14], src, C(5), None, ALU.mult, None, [tok, "c5"], ["NBp%d" % w])
-        vts(T["NB%d" % w][:, 14:16], src, C(2), None, ALU.mult, None, [tok, "c2"], ["NBq%d" % w])
-
     fill(T.ONE[:, :], 1.0, ["ONE"])
     iota(T.IP[:, :], [[0, 1]], 0, 1, ["IP"])
-    iotaf(T.R0[:, :], [[1, 16], [0, 16]], ENT, 0, ["R0"])
-    iotaf(T.BI[:, :], [[8, 20]], 0, 0, ["BI"])
     iota(T.CI[:, 0:8], [[224, 8]], 0, 0, ["CI0"])
     iota(T.CI[:, 8:16], [[0, 4], [224, 2]], 0, 0, ["CI1"])
+    iotaf(T.R0[:, :], [[1, 16], [0, 16]], ENT, 0, ["R0"])
+    iotaf(T.BI[:, :], [[-8, 20]], col(0) + ENT, 0, ["BI"])
     sel(T.ID[:, :], T.ONE[:, 0:128], [[-1, 128]], ALU.is_equal, 0, 1, ["ONE"], ["ID"])
     sel(T.G1[:, :], T.ONE[:, 0:8], [[-16, 8]], ALU.is_ge, 0, 1, ["ONE"], ["G1"])
     sel(T.G2[:, :], T.G1[:, :], [[16, 8]], ALU.is_ge, 14, -1, ["G1"], ["G2"])
     act(T.B1[:, NODE + 1792:2240], T.ONE[:, 0:256], ["ONE"], ["B1z"], 0.0, None, ACT.Silu)
     for b in range(0, NA, 2):
         n = 128 * min(2, NA - b)
-        act(T.SA[:, 128 * b:128 * b + n], T.R0[:, 0:n], ["R0", "BI"], ["SA%d" % b], 1.0, T.BI[:, (col(b) - ENT) // 8:(col(b) - ENT) // 8 + 1], ACT.Silu)
+        act(T.SA[:, 128 * b:128 * b + n], T.R0[:, 0:n], ["R0", "BI"], ["SA%d" % b], -1.0, T.BI[:, b:b + 1])
     vts(T.IT[:, 1:2], T.IP[:, :], 3, 1, ALU.logical_shift_right, ALU.bitwise_and, ["IP"], ["IT1"])
     vts(T.IT[:, 0:1], T.IP[:, :], 15, None, ALU.bitwise_and, None, ["IP"], ["IT0"])
-    vts(T.IT[:, 2:3], T.IP[:, :], 31, None, ALU.bitwise_and, None, ["IP"], ["IT2"])
     vts(C(3), T.IT[:, 1:2], 112.0, None, ALU.mult, None, ["IT1"], ["c3"])
     vts(C(0), T.IT[:, 0:1], 14.5, None, ALU.is_lt, None, ["IT0"], ["c0"])
-    vts(C(4), T.IT[:, 2:3], float(ENT), None, ALU.add, None, ["IT2"], ["c4"])
-    vts(C(6), T.IT[:, 2:3], ENT - 16.0, None, ALU.add, None, ["IT2"], ["c6"])
-    vcopy(C(2), T.IT[:, 1:2], ["IT1"], ["c2"])
-    vts(C(5), T.IT[:, 1:2], -1.0, 1.0, ALU.mult, ALU.add, ["IT1"], ["c5"])
-    vts(C(1), C(0), -2.0, 2.0, ALU.mult, ALU.add, ["c0"], ["c1"])
-    fill(T.B0[:, NODE + 1792:2240], 0.0, ["B0z"])
-    fill(T.BWV[:, :], 0.0, ["BWV"])
-    vts(T.EP[:, 0:256], T.R0[:, :], C(4), None, ALU.is_equal, None, ["R0", "c4"], ["EP0"])
-    vts(T.EP[:, 256:512], T.R0[:, :], C(6), None, ALU.is_equal, None, ["R0", "c6"], ["EP1"])
     vts(T.CLf[:, 0:8], T.CI[:, 0:8], C(3), None, ALU.add, None, ["CI0", "c3"], ["CLf0"])
+    vts(C(1), C(0), -2.0, 2.0, ALU.mult, ALU.add, ["c0"], ["c1"])
     vts(T.CLf[:, 8:16], T.CI[:, 8:16], C(3), None, ALU.add, None, ["CI1", "c3"], ["CLf1"])
-    vcopy(T.FRF[:, :], T.FRI[:, :], ["FRI"], ["FRF"])
-    vtt(T.LF[:, 0:8], T.FRF[:, :], T.CLf[:, 0:8], ALU.add, ["FRF", "CLf0"], ["LF0"])
-    vtt(T.LF[:, 8:16], T.FRF[:, :], T.CLf[:, 8:16], ALU.add, ["FRF", "CLf1"], ["LF1"])
-    places(0, T.FRF[:, 0:2], "FRF")
-    vcopy(T.LIST[:, 0:8], T.LF[:, 0:8], ["LF0"], ["LIST"])
-    vcopy(T.LISTC[:, :], T.LF[:, 8:16], ["LF1"], ["LISTC"])
-    vts(T.ID2[:, :], T.ID[:, :], 2.0, None, ALU.mult, None, ["ID"], ["ID2"])
-    vts(T.BWV[:, 15:128:16], T.G2[:, :], -1.0 / 16, None, ALU.mult, None, ["G2", "BWV"], ["BWV"])
-    if any(c[3] == "A" for c in CH):
-        fill(C(9), 0.5, ["c9"])
-        fill(T.BWA[:, :], 0.0, ["BWA"])
-        vts(T.EN[:, :], T.EP[:, :], -1.0, None, ALU.mult, None, ["EP0", "EP1"], ["EN"])
-        vts(T.BWA[:, 15:128:16], T.G2[:, :], -1.0 / 32, None, ALU.mult, None, ["G2", "BWA"], ["BWA"])
 
-    def reset(n, w, lo=0, hi=1792):
-        if n == 0:
-            iotaf(T["IA%d" % (w % 2)][:, 2 * lo:2 * hi:2], [[1, hi - lo]], NODE + lo, 0, ["IA%d" % (w % 2)])
-        else:
-            iotaf(T["IV%d" % (w % 2)][:, 2 * lo:2 * hi:2], [[0, hi - lo]], int(NONE), 0, ["IV%d" % (w % 2)])
+    def places(w, src, tok):
+        vcopy(T["NB%d" % w][:, 14:16], src, [tok], ["NBp%d" % w])
 
-    def late_gpsimd():
-        for d in range(4):
-            iota(T.UPG[:, 120 * d + 112:120 * d + 120], [[16, 8]], 1792, 1, ["UPGp%d" % d])
-        sel(T.EG[:, :], T.ONE[:, 0:512], [[40, 4], [1, 8], [0, 16]], ALU.is_equal, 0, -1, ["ONE"], ["EG"])
-        sel(T.SEL[:, :], T.ONE[:, 0:8], [[-16, 8]], ALU.is_equal, -15, 1, ["ONE"], ["SEL"])
-        gcopy(T.SELF[:, :], T.SEL[:, :], 8, ["SEL"], ["SELF"])
-        sel(T.TRI[:, 0:120], T.ONE[:, 0:120], [[1, 120]], ALU.is_ge, 0, -1, ["ONE"], ["TRI0"])
-        sel(T.TRI[:, 120:121], T.ONE[:, 0:1], [[0, 1]], ALU.is_ge, 111, -1, ["ONE"], ["TRI1"])
-        iota(T.UPW[:, 1792:1920], [[0, 8], [16, 16]], 1792, 1, ["UPWp"])
+    def first_lists():
+        vcopy(T.FRF[:, :], T.FRI[:, :], ["FRI"], ["FRF"])
+        places(0, T.FRI[:, 0:2], "FRI")
+        vtt(T.LF[:, 0:8], T.FRF[:, :], T.CLf[:, 0:8], ALU.add, ["FRF", "CLf0"], ["LF0"])
+        vtt(T.LF[:, 8:16], T.FRF[:, :], T.CLf[:, 8:16], ALU.add, ["FRF", "CLf1"], ["LF1"])
+        vcopy(T.LIST[:, 0:8], T.LF[:, 0:8], ["LF0"], ["LIST"])
+        vcopy(T.LISTC[:, :], T.LF[:, 8:16], ["LF1"], ["LISTC"])
+
+    def reset(w, lo=0, hi=1792):
+        iotaf(T["IA%d" % (w % 2)][:, 2 * lo:2 * hi:2], [[1, hi - lo]], NODE + lo, 0, ["IA%d" % (w % 2)])
+
+    def for_counts():
+        fill(T.B0[:, NODE + 1792:2240], 0.0, ["B0z"])
+        fill(T.BWV[:, :], 0.0, ["BWV"])
+        vts(T.ID2[:, :], T.ID[:, :], 2.0, None, ALU.mult, None, ["ID"], ["ID2"])
+        vts(T.BWV[:, 15:128:16], T.G2[:, :], -1.0 / 16, None, ALU.mult, None, ["G2", "BWV"], ["BWV"])
 
     def vector_values():
         for b in range(NA, 20, 2):
             n = 128 * min(2, 20 - b)
-            vts(T.SV[:, 128 * b:128 * b + n], T.R0[:, 0:n], float(col(b) - ENT), None, ALU.add, None, ["R0"], ["SV%d" % b])
+            vts(T.SV[:, 128 * b:128 * b + n], T.R0[:, 0:n], -1.0, float(col(b) + ENT), ALU.mult, ALU.add, ["R0"], ["SV%d" % b])
 
-    def ghost_constants():
+    def for_ghosts():
+        vcopy(C(2), T.IT[:, 1:2], ["IT1"], ["c2"])
+        vts(C(5), T.IT[:, 1:2], -1.0, 1.0, ALU.mult, ALU.add, ["IT1"], ["c5"])
         vts(T.CG[:, 0:1], T.IT[:, 1:2], 120.0, None, ALU.mult, None, ["IT1"], ["CG0"])
         vts(T.CG[:, 1:2], T.IT[:, 1:2], 120.0, 240.0, ALU.mult, ALU.add, ["IT1"], ["CG1"])
-
-    def columns():
         fill(C(11), float(NODE), ["c11"])
-        fill(C(12), 256.0, ["c12"])
-        fill(C(8), -MAGIC, ["c8"])
-        vts(C(13), T.IP[:, :], -MAGIC - 128.0, MAGIC, ALU.mult, ALU.add, ["IP"], ["c13"])
+        vts(T.IDL[:, :], T.ID[:, :], C(5), None, ALU.mult, None, ["ID", "c5"], ["IDL"])
+        vts(T.IDU[:, :], T.ID[:, :], C(2), None, ALU.mult, None, ["ID", "c2"], ["IDU"])
+
+    def ghost_fill():
+        for d in range(4):
+            iota(T.UPG[:, 120 * d + 112:120 * d + 120], [[16, 8]], 1792, 1, ["UPGp%d" % d])
+
+    def for_turns():
+        for t in ("SEL", "SELF", "SELH"):
+            sel(T[t][:, 0:8], T.ONE[:, 0:8], [[-16, 8]], ALU.is_equal, -15, 1, ["ONE"], [t + "0" * (t == "SEL")])
+
+    def for_lists():
+        iota(T.UPW[:, 1792:1920], [[0, 8], [16, 16]], 1792, 1, ["UPWp"])
+        sel(T.TRI[:, :], T.ONE[:, 0:128], [[1, 128]], ALU.is_ge, 0, -1, ["ONE"], ["TRI"])
+        sel(T.LX[:, :, :], T.ONE[:, :], [[0, 528]], ALU.is_gt, 0, 0, ["ONE"], ["LXz"])
+        iotaf(T.UPR[0:1, 112:120], [[1, 8]], 1, 0, ["UPR"])
+        for t in ("B0", "B1"):
+            sel(T[t][:, 0:ENT], T.ONE[:, 0:ENT], [[0, ENT]], ALU.is_gt, 0, 0, ["ONE"], [t + "y"])
+
+    def for_sums():
+        for t, c in (("IDO", 0.5), ("IDH", HALF), ("IDM", -float(NODE)), ("IDF", 1.0)):
+            vts(T[t][:, :], T.ID[:, :], c, None, ALU.mult, None, ["ID"], [t])
+        vts(T.CM[0:2, :], T.ONE[0:2, 0:128], T.COL[0:2, 13:14], None, ALU.mult, None, ["ONE", "c13"], ["CM"])
+        vcopy(T.CL[:, 0:8], T.CLf[:, 0:8], ["CLf0"], ["CL0"])
+        vcopy(T.CL[:, 8:10], T.CLf[:, 0:2], ["CLf0"], ["CL1"])
+        fill(T.CL[:, 10:12], 0.0, ["CL2"])
+
+    def for_frontiers():
         vts(C(7), T.IP[:, :], 120.0, None, ALU.is_equal, None, ["IP"], ["c7"])
         vts(T.WV[:, :], T.CI[:, 0:8], -1.0, 1679.0, ALU.mult, ALU.add, ["CI0"], ["WV"])
         fill(T.RW[:, :], 0.0, ["RW"])
-
-    def late_scalar():
-        act(T.FT[:, :], T.ONE[:, 0:128], ["ONE"], ["FT"])
-        for p in (0, 1):
-            act(T["B%d" % p][:, 0:ENT], T.ONE[:, 0:ENT], ["ONE"], ["B%dy" % p], 0.0)
-        act(T.CL[:, 0:8], T.CLf[:, 0:8], ["CLf0"], ["CL0"])
-        act(T.CL[:, 8:10], T.CLf[:, 0:2], ["CLf0"], ["CL1"])
-        act(T.CL[:, 10:12], T.ONE[:, 0:2], ["ONE"], ["CL2"], 0.0)
-        act(T.IDM[:, :], T.ID[:, :], ["ID"], ["IDM"], -float(NODE))
-        act(T.IDO[:, :], T.ID[:, :], ["ID"], ["IDO"], 0.5)
-        act(T.CM[0:2, :], T.ONE[0:2, 0:128], ["ONE", "c13"], ["CM"], T.COL[0:2, 13:14])
-
-    def late_vector():
-        vts(T.IDH[:, :], T.ID[:, :], HALF, None, ALU.mult, None, ["ID"], ["IDH"])
-        vcopy(T.IDF[:, :], T.ID[:, :], ["ID"], ["IDF"])
-        vts(T.LX[:, :, :], T.ONE[:, :], 0.0, None, ALU.mult, None, ["ONE"], ["LXz"])
+        vts(C(13), T.IP[:, :], -MAGIC - 128.0, MAGIC, ALU.mult, ALU.add, ["IP"], ["c13"])
         vts(T.RW[:, 0:96:13], T.WV[:, :], C(7), 1.0, ALU.mult, ALU.add, ["WV", "c7", "RW"], ["RW"])
+        fill(C(8), -MAGIC, ["c8"])
         vts(T.RW[:, 10:24:13], T.ONE[:, 0:2], C(7), None, ALU.subtract, None, ["ONE", "c7", "RW"], ["RW"])
+        fill(C(12), 256.0, ["c12"])
         vts(T.RW[:, 8:22:13], T.RW[:, 10:24:13], 113.0, -112.0, ALU.mult, ALU.add, ["RW"], ["RW"])
+        fill(T.UPR[0:1, :], 0.0, ["UPR"])
+
+    def no_offers():
+        fill(C(14), NONE, ["c14"])
+        fill(T.IV[:, 0:2 * FILL:2], NONE, ["IV"])
+        act(T.IV[:, 2 * FILL:3584:2], T.SA[:, 0:1792 - FILL], ["c14"] + ["SA%d" % b for b in range(0, NA, 2)], ["IVa"], 0.0, C(14))
+
+    def scales():
+        for w in range(1, WAVES):
+            fill(T.SC[:, 128 * w:128 * w + 128], 1.0 / STEP ** w, ["SC%d" % w])
+            vts(T.SEL[:, 8 * w:8 * w + 8], T.SEL[:, 0:8], float(STEP ** w), None, ALU.mult, None, ["SEL0"], ["SEL%d" % w])
 
     def marks(n, w):
-        if w == 0:
-            mm([(T.psX1[0:112, turned(b)], tab(w)[:, NODE + 112 * b:NODE + 112 * b + 112], T.SEL[:, :], True, True) for b in range(16)],
-               nodes_of(w) + ["SEL"], ["psX1"])
+        if n == 0:
+            mm([(T.psX1[0:112, turned(b)], tab(w)[:, NODE + 112 * b:NODE + 112 * b + 112], T.SEL[:, 0:8], True, True) for b in range(16)],
+               nodes_of(w) + ["SEL0"], ["psX1"])
             act(T.THR[0:112, :], T.psX1[0:112, 0:128], ["psX1", "c11"], ["THR"], -float(NODE), T.COL[0:112, 11:12])
-        elif w + 1 < WAVES:
-            o = T.psX1[0:112, 0:128]
-            mm([(o, T.ID[0:112, 0:112], T.THR[0:112, :], True, False), (o, T.IDM[0:112, 0:112], T.FT[0:112, :], False, True)],
-               ["ID", "IDM", "THR", "FT"], ["psX1"])
-            act(T.THR[0:112, :], o, ["psX1"], ["THR"])
+        elif not last(w):
+            o = T.psX0[0:112, 128:256]
+            mm([(o, T.ID[0:112, 0:112], T.THR[0:112, :], True, w == 0)]
+               + [(o, T.IDM[0:112, 0:112], T["FT%d" % k][0:112, :], False, k == w - 1) for k in range(w)],
+               ["ID", "IDM", "THR"] + ["FT%d" % k for k in range(w)], ["psX0"])
+
+    def entry_notes(i, w):
+        if i == 4:
+            return T.GL[:, 4 * w:4 * w + 4, MID:MID + 8], ["GL%d" % w]
+        return T["NB%d" % w][:, 16 + 32 * i:48 + 32 * i], ["NB%s%d" % ("n" if i else "z", w)]
+
+    def window(w):
+        return tab(w)[:, NODE:2240], nodes_of(w) + [name(w) + "z"]
 
     def gather(i, w):
-        a, b, q = CH[i][:3]
-        copy(q, T.Q[:, 128 * a:128 * b], tab(w)[:, NODE:2240].indirect(T.P16[:, 8 * a:8 * b]),
-             nodes_of(w) + ["B%dz" % (w % 2), "P%d" % i], ["Q%d" % i])
-
-    turn = [0]
-    bank_of = {}
+        (a, b), (win, R) = PIECES[i], window(w)
+        copy((GATHER if w else GATHER0)[i], T.Q[:, 16 * a:16 * b], win.indirect(T.P16[:, a:b]), R + ["P%d" % (a // 32)], ["Q%d" % i])
 
     def spread(i, w):
-        a, b, _, q = CH[i]
-        ps = "psD%d" % (turn[0] % 2)
-        turn[0] += 1
-        bank_of[i] = ps
-        k, x, n = a // 4 * 32, 128 * (a % 4), 128 * (b - a)
-        if a >= 16:
-            mm([(T[ps][:, 0:n], T.nTg[:, :], T.EG[:, x:x + n], True, True)], ["EG", "nTg"], [ps])
-        elif q == "V":
-            mm([(T[ps][:, 0:n], T.nT[k:k + 32, :], T.EP[k:k + 32, x:x + n], True, True)], ["EP0", "EP1", "nT"], [ps])
-        else:
-            mm([(T[ps][:, 0:n], T.nT[k:k + 32, :], T.EN[k:k + 32, x:x + n], True, False), (T[ps][:, 0:n], T.ID[:, :], T.Q[:, 128 * a:128 * b], False, True)],
-               ["Q%d" % i, "ID", "EN", "nT"], [ps])
+        src, R = entry_notes(i, w)
+        ps = "ps" + DBANK[i]
+        mm([(T[ps][:, t:512:16], T.ID[:, :], src, True, True) for t in range(16)], R + ["ID"], [ps])
 
     def compare(i, w):
-        a, b, _, q = CH[i]
-        n, ps = 128 * (b - a), bank_of[i]
-        if q == "V":
-            vtt(T.SG[:, 128 * a:128 * b], T.Q[:, 128 * a:128 * b], T[ps][:, 0:n], ALU.is_ge, [ps, "Q%d" % i], ["SG%d" % i])
-        else:
-            act(T.SG[:, 128 * a:128 * b], T[ps][:, 0:n], [ps, "c9"], ["SG%d" % i], 1.0, C(9), ACT.Sign)
+        a, b = PIECES[i]
+        ps, x = "ps" + DBANK[a // 32], 16 * (a % 32)
+        vtt(T.SG[:, 16 * a:16 * b], T.Q[:, 16 * a:16 * b], T[ps][:, x:x + 16 * (b - a)], ALU.is_ge, [ps, "Q%d" % i], ["SG%d" % i])
 
-    def cols(gi):
-        return 8 * CH[GR[gi][0]][0], 8 * CH[GR[gi][-1]][1], "psY%d" % (gi % 2), CH[GR[gi][0]][3]
+    def count(i, w):
+        (a, b), ps = PIECES[i], "ps" + CBANK[i]
+        out = T[ps][:, a:b]
+        mm([(out, T.ID2[:, :], T.Pf[:, a:b], True, False)]
+           + [(out, T.BWV[:, 15 - k:143 - k], T.SG[:, 16 * a + k:16 * b:16], False, k == 15) for k in range(16)],
+           ["ID2", "BWV", "Pf%d" % (a // 32), "SG%d" % i], [ps])
 
-    def count(gi, w):
-        lo, hi, ps, q = cols(gi)
-        out = T[ps][:, 0:hi - lo]
-        mm([(out, T.ID2[:, :], T.Pf[:, lo:hi], True, False)]
-           + [(out, T["BW" + q][:, 15 - k:143 - k], T.SG[:, 16 * lo + k:16 * hi:16], False, k == 15) for k in range(16)],
-           ["ID2", "BW" + q] + ["Pf%d" % i for i in GR[gi]] + ["SG%d" % i for i in GR[gi]], [ps])
+    def offsets(i, w):
+        (a, b), ps = PIECES[i], "ps" + CBANK[i]
+        vts(T.OFFS[:, a:b], T[ps][:, a:b], 1.03125, None, ALU.add, None, [ps], ["OF%d" % i])
 
-    def offsets(gi, w):
-        lo, hi, ps, q = cols(gi)
-        vts(T.OFFS[:, lo:hi], T[ps][:, 0:hi - lo], 0.5625 if q == "A" else 1.03125, None, ALU.add, None, [ps], ["OF%d" % gi])
-
-    def scatter(b, w):
-        gi = [k for k in range(len(GR)) if cols(k)[0] <= 8 * b < cols(k)[1]][0]
-        off = T.OFFS[:, 8 * b:8 * b + 8]
-        if b < NA:
+    def scatter(c, w):
+        off = T.OFFS[:, 8 * c:8 * c + 8]
+        R = ["OF%d" % i for i, (a, b) in enumerate(PIECES) if a <= 8 * c < b]
+        if c < NA:
             t = "IA%d" % (w % 2)
-            op("A", lambda a: a.activation(T[t][:, :].indirect(off), T.SA[:, 128 * b:128 * b + 128], ACT.Silu),
-               ["OF%d" % gi, "SA%d" % (b // 2 * 2), t], [t])
+            op("A", lambda a: a.activation(T[t][:, :].indirect(off), T.SA[:, 128 * c:128 * c + 128], ACT.Silu), R + ["SA%d" % (c // 2 * 2)], [t])
+        elif w == 0:
+            vcopy(T.IV[:, :].indirect(off), T.SV[:, 128 * c:128 * c + 128], R + ["SV%d" % (c - (c - NA) % 2), "IVa"], ["IV"])
         else:
-            t = "IV%d" % (w % 2)
-            vcopy(T[t][:, :].indirect(off), T.SV[:, 128 * b:128 * b + 128], ["OF%d" % gi, "SV%d" % (b - (b - NA) % 2), t], [t])
+            vtt(T.IV[:, :].indirect(off), T.SV[:, 128 * c:128 * c + 128], T.SC[:, 128 * w:128 * w + 128], ALU.mult, R + ["SC%d" % w], ["IV"])
 
-    def turn_table(kind, ps, banks, w):
-        t = "I%s%d" % (kind, w % 2)
-        s = "SELF" if kind == "A" else "SEL"
-        mm([(T[ps][0:112, turned(b)], T[t][:, 224 * b:224 * b + 224:2], T[s][:, :], True, True) for b in banks], [t, s], [ps, "T%s%d" % (kind, banks[0])])
+    def turn_table(t, s, step, ps, quarters, w=0):
+        mm([(T[ps][0:112, turned(b)], T[t][:, step * 112 * b:step * 112 * (b + 1):step], T[s][:, 8 * w:8 * w + 8], True, True)
+            for b in range(4 * quarters[0], 4 * quarters[-1] + 4)], [t if step == 2 else "IH%d" % quarters[0], s + str(w) * (s == "SEL")], [ps])
+
+    def narrow(i, w):
+        t = "IA%d" % (w % 2)
+        if i in NARROW:
+            act(T.IH[:, 448 * i:448 * i + 448], T[t][:, 896 * i:896 * i + 896:2], [t], ["IH%d" % i])
 
     def scalar_table(n, w):
-        if n < 4:
-            turn_table("A", "psX1", range(4 * n, 4 * n + 4), w)
+        if n == 4:
+            vcopy(T.LA[0:112, :], T.psX1[0:112, 0:128], ["psX1"], ["LA"])
+        elif n in NARROW:
+            turn_table("IH", "SELH", 1, "psX1", [n])
         else:
-            act(T.LA[0:112, :], T.psX1[0:112, 0:128], ["psX1"] + ["TA%d" % b for b in range(0, 16, 4)], ["LA"])
+            turn_table("IA%d" % (w % 2), "SELF", 2, "psX1", [n])
 
     def pf(ks):
-        a, b = 8 * CH[ks[0]][0], 8 * CH[ks[-1]][1]
+        a, b = 32 * ks[0], 32 * ks[-1] + 32
         vcopy(T.Pf[:, a:b], T.P16[:, a:b], ["P%d" % k for k in ks], ["Pf%d" % k for k in ks])
 
     def parents():
-        vcopy(T.P16[:, 0:128], T.UPW[:, :].indirect(T.LIST[:, 0:8]), ["LIST", "UPWp"] + ["UPW%d" % i for i in range(4)], ["P%d" % k for k in own])
+        vcopy(T.P16[:, 0:128], T.UPW[:, :].indirect(T.LIST[:, 0:8]), ["LIST", "UPWp"] + ["UPW%d" % i for i in range(4)], ["P%d" % k for k in range(4)])
+
+    start = lambda d: MID - 2 - 8 * d
 
     def send(w):
         dst = [T.cores[(rank + d) % N] for d in range(1, 5)]
@@ -415,73 +416,56 @@ def rank_program(g, core, T, topo):
         for c in dst:
             rid, pid = topo.addr(c, core)
             ids.append(DstId(rid=rid, pnc=pid))
-        ready("G", ["NBz%d" % w, "NBp%d" % w, "NBq%d" % w])
+        ready("G", ["NBz%d" % w, "NBp%d" % w])
         g.remote_dma_fused([RemoteDMATransfer(
-            dst_ids=ids, dma_engine_mask=m, remote_sem=T.sem["arr%d" % w], srcs=[T["NB%d" % w][:, 12:48]],
-            dsts=[T.GL[:, (4 * w + d) * SLOT:(4 * w + d) * SLOT + 36] for d in range(4)])], local_sem=T.sem["lsem"])
+            dst_ids=ids, dma_engine_mask=m, remote_sem=T.sem["arr%d" % w], srcs=[T["NB%d" % w][:, 14:48]],
+            dsts=[T.GL[:, 4 * w + d, start(d):start(d) + 34] for d in range(4)])], local_sem=T.sem["lsem"])
         arrive("GL%d" % w, "arr%d" % w, 4 * ne)
         engines[0] = ne
 
     engines = [0]
 
-    def notes(q, out, win, R, W):
-        if q == "V":
-            vts(out, win, C(0), C(1), ALU.mult, ALU.add, R + ["c0", "c1"], W)
-        else:
-            act(out, win, R + ["c0", "c1"], W, C(0), C(1))
-
     def sent_notes(w):
         x = 8 if w else 0
-        notes(ZQ, T["NB%d" % w][:, 16:48], tab(w)[:, NODE:NODE + 448].indirect(T.LIST[:, x:x + 2]), nodes_of(w)[:1] + ["LIST"], ["NBz%d" % w])
+        vts(T["NB%d" % w][:, 16:48], tab(w)[:, NODE:NODE + 448].indirect(T.LIST[:, x:x + 2]), C(0), C(1), ALU.mult, ALU.add,
+            nodes_of(w)[:1] + ["LIST", "c0", "c1"], ["NBz%d" % w])
 
     def entries(n, w):
-        notes("A", T["NB%d" % w][:, 48:144], tab(w)[:, NODE:2240].indirect(T.LIST[:, 2:8]), nodes_of(w) + ["B%dz" % (w % 2), "LIST"], ["NBn%d" % w])
-
-    def entries_turned(n, w):
-        mm([(T.psX0[:, 0:128], T["NB%d" % w][:, 16:144], T.ID[:, :], True, True)], ["NBn%d" % w, "NBz%d" % w, "ID"], ["psX0"])
-        act(T.nT[:, :], T.psX0[:, 0:128], ["psX0"], ["nT"])
+        win, R = window(w)
+        act(T["NB%d" % w][:, 48:144], win.indirect(T.LIST[:, 2:8]), R + ["LIST", "c0", "c1"], ["NBn%d" % w], C(0), C(1))
 
     def ghosts(n, w):
-        s0 = 4 * w * SLOT
         if n == 0:
-            for x in range(2):
-                s = s0 + 2 * x * SLOT + x
-                vts(T.LISTG[:, x:x + 1], T.GL[:, s:s + 1], T.GL[:, s + SLOT + 2:s + SLOT + 3], T.CG[:, x:x + 1], ALU.add, ALU.add,
-                    ["CG%d" % x, "GL%d" % w], ["LISTG%d" % x])
+            place = lambda d: T.GL[:, 4 * w + d, start(d) + d // 2:start(d) + 1 + d // 2]
+            mm([(T.psX0[:, 0:2], T.ID[:, :], T.CG[:, :], True, False)]
+               + [(T.psX0[:, d // 2:d // 2 + 1], T[("IDL", "IDU")[d % 2]][:, :], place(d), False, d == 3) for d in range(4)],
+               ["ID", "IDL", "IDU", "CG0", "CG1", "GL%d" % w], ["psX0"])
         elif n == 1:
-            vcopy(T.P16[:, 128:160], T.UPG[:, :].indirect(T.LISTG[:, :]), ["LISTG0", "LISTG1", "UPG"] + ["UPGp%d" % d for d in range(4)],
-                  ["P%d" % k for k in far])
+            vcopy(T.LISTG[:, :], T.psX0[:, 0:2], ["psX0"], ["LISTG"])
         elif n == 2:
-            mm([(T.psX0[32 * d:32 * d + 32, 0:128], T.GL[:, s0 + d * SLOT + 4:s0 + d * SLOT + 36], T.ID[:, :], True, True) for d in range(4)],
-               ["ID", "GL%d" % w], ["psX0"])
-        elif n == 3:
-            copy(GQ, T.nTg[:, :], T.psX0[:, 0:128], ["psX0"], ["nTg"])
+            vcopy(T.P16[:, 128:160], T.UPG[:, :].indirect(T.LISTG[:, :]), ["LISTG", "UPG"] + ["UPGp%d" % d for d in range(4)], ["P4"])
         else:
-            pf(far)
+            pf([4])
 
     def into_table(n, w):
-        e, NBt = ents_of(w), T["NB%d" % w]
-        gcopy(tab(w)[:, col(NA):col(16)], NBt[:, 16 + 8 * NA:144], 128 - 8 * NA, ["NBn%d" % w, "NBz%d" % w], [e[4]])
-        gcopy(tab(w)[:, col(0):col(0) + 8 * NA], NBt[:, 16:16 + 8 * NA], 8 * NA, ["NBn%d" % w, "NBz%d" % w], [e[5]])
-        for d in range(4):
-            s = (4 * w + d) * SLOT + 4 + 8 * d
-            gcopy(tab(w)[:, col(16 + d):col(16 + d) + 8], T.GL[:, s:s + 8], 8, ["GL%d" % w], [e[d]])
+        e = ents_of(w)
+        gcopy(tab(w)[:, col(0):col(16):-1], T["NB%d" % w][:, 16:144], 128, ["NBn%d" % w, "NBz%d" % w], [e[0]])
+        gcopy(tab(w)[:, col(16):col(20):-1], entry_notes(4, w)[0], 32, ["GL%d" % w], [e[1]])
 
     SUM = ["psS0", "psS1", "psD0", "psD1"]
-
-    rounder = lambda i, w: (RQ if w + 1 < WAVES else RL)[i]
     LEAST = ["psX0", "psY0"]
     TURN = ["psY1", "psX1"]
+    rounder = lambda i, w: (RL if last(w) else RQ)[i]
 
     def turn_list(i, w):
-        ps = TURN[i % 2]
-        mm([(T[ps][:, 0:28], T.LX[0:112, 32 * i + 3 - r:32 * i + 35 - r, :], T.IDF[0:112, r:112:4], r == 0, r == 3) for r in range(4)],
+        ps = TURN[i // 2]
+        mm([(T[ps][:, 28 * i:28 * i + 28], T.LX[0:112, 32 * i + 3 - r:32 * i + 35 - r, :], T.IDF[0:112, r:112:4], r == 0, r == 3) for r in range(4)],
            ["LX%d" % (i // 2), "IDF"], [ps])
 
     def winners(i, w):
         out, win = T.W[:, 448 * i:448 * i + 448], tab(w)[:, 0:NODE + 1792].indirect(T.L16[:, 28 * i:28 * i + 28])
-        R = nodes_of(w) + ents_of(w) + ["B%dy" % (w % 2), "L16%d" % i]
-        if (WQ if w + 1 < WAVES else WL)[i] == "V":
+        R = nodes_of(w) + ents_of(w) + [name(w) + "y", "L16%d" % i]
+        if (WL if last(w) else WQ)[i] == "V":
             vts(out, win, 256.0, None, ALU.add, None, R, ["W%d" % i])
         else:
             act(out, win, R + ["c12"], ["W%d" % i], 1.0, C(12))
@@ -489,49 +473,47 @@ def rank_program(g, core, T, topo):
     def old_half(i, w):
         o = T[SUM[i]][:, 0:448]
         mm([(o, T.CM[0:2, :], T.ONE[0:2, 0:448], True, False)] * (rounder(i, w) == "A")
-           + [(o, T.IDO[:, :], tab(w)[:, NODE + 448 * i:NODE + 448 * i + 448], rounder(i, w) == "V", False)], ["IDO", "CM", "ONE", nodes_of(w)[i]], [SUM[i]])
+           + [(o, T.IDO[:, :], nodes(w, i), rounder(i, w) == "V", False)], ["IDO", "CM", "ONE", nodes_of(w)[i]], [SUM[i]])
 
     def new_half(i, w):
         ps = T[SUM[i]]
         mm([(ps[:, 112 * j:112 * j + 112], T.IDH[:, :], T.W[:, 448 * i + lane(j):448 * i + 448:4], False, j == 3) for j in range(4)],
-           ["IDH", SUM[i], "W%d" % i], [SUM[i]])
+           ["IDH", "W%d" % i], [SUM[i]])
 
     def round_down(i, w):
-        out, tok = tab(w + 1)[:, NODE + 448 * i:NODE + 448 * i + 448], nodes_of(w + 1)[i]
+        out, tok, o = nodes(w + 1, i), nodes_of(w + 1)[i], T[SUM[i]][:, 0:448]
         if rounder(i, w) == "V":
-            vts(out, T[SUM[i]][:, 0:448], MAGIC - 128.0, -MAGIC, ALU.add, ALU.add, [SUM[i]], [tok])
+            vts(out, o, MAGIC - 128.0, -MAGIC, ALU.add, ALU.add, [SUM[i]], [tok])
         else:
-            act(out, T[SUM[i]][:, 0:448], [SUM[i], "c8"], [tok], 1.0, C(8))
-        if w + 1 == WAVES:
+            act(out, o, [SUM[i], "c8"], [tok], 1.0, C(8))
+        if last(w):
             op("S", lambda s: s.dma_start(T.y[:, 448 * i:448 * i + 448], out), [tok], ["y%d" % i], "out%d" % i, 16)
 
     def tail(t, w):
         k, n = t[0], int(t[1:])
         if k == "x":
-            turn_table("V", LEAST[n], range(8 * n, 8 * n + 8), w)
+            turn_table("IV", "SEL", 2, LEAST[n], [2 * n, 2 * n + 1], w)
         elif k == "m":
             vtt(T.LX[0:112, 64 * n + 3:64 * n + 67:4, :], T[LEAST[n]][0:112, 64 * n:64 * n + 64], T.LA[0:112, 64 * n:64 * n + 64], ALU.min,
                 [LEAST[n], "LA", "LXz"], ["LX%d" % n])
         elif k == "t":
             turn_list(n, w)
         elif k == "l":
-            vcopy(T.L16[:, 28 * n:28 * n + 28], T[TURN[n % 2]][:, 0:28], [TURN[n % 2]], ["L16%d" % n])
+            vcopy(T.L16[:, 56 * n:56 * n + 56], T[TURN[n]][:, 56 * n:56 * n + 56], [TURN[n]], ["L16%d" % (2 * n), "L16%d" % (2 * n + 1)])
         elif k == "w":
             winners(n, w)
-        elif k == "a":
-            old_half(n, w)
         elif k == "b":
             new_half(n, w)
         elif k == "r":
             round_down(n, w)
-        elif w + 1 == WAVES:
-            return
         elif k == "F":
-            vtt(T.FT[0:112, :], T.LX[0:112, 3:131:4, :], T.THR[0:112, :], ALU.is_lt, ["LX0", "LX1", "THR"], ["FT"])
+            vtt(T["FT%d" % w][0:112, :], T.LX[0:112, 3:131:4, :], T.psX0[0:112, 128:256], ALU.is_lt, ["LX0", "LX1", "psX0"], ["FT%d" % w])
         elif k == "c":
-            mm([(T.psY0[0:121, 0:128], T.TRI[0:120, 0:121], T.FT[0:120, :], True, True)], ["TRI0", "TRI1", "FT"], ["psY0"])
+            o = T.psY0[0:121, 0:128]
+            mm([(o, T.UPR[0:1, 0:121], T.ONE[0:1, 0:128], True, False), (o, T.TRI[0:112, 0:121], T["FT%d" % w][0:112, :], False, True)],
+               ["TRI", "UPR", "ONE", "FT%d" % w], ["psY0"])
         elif k == "u":
-            copy(UQ, T.CUM[0:121, :, :, :], T.psY0[0:121, 0:128], ["psY0"], ["CUM"])
+            vcopy(T.CUM[0:121, :, :, :], T.psY0[0:121, 0:128], ["psY0"], ["CUM"])
         elif k == "k":
             for j in range(8):
                 vts(T.OKB[0:121, :, j:128:8, :], T.CUM[0:121, :, :, :], j + 0.5, None, ALU.is_lt, None, ["CUM"], ["OK%d" % j])
@@ -541,6 +523,7 @@ def rank_program(g, core, T, topo):
                ["ID", "CL0", "CL1", "CL2", "RW"] + ["OK%d" % j for j in range(8)], ["psX0"])
         elif t == "L1":
             vcopy(T.LIST[:, :], T.psX0[:, 0:10], ["psX0"], ["LIST"])
+        elif t == "L2":
             places(w + 1, T.psX0[:, 10:12], "psX0")
         elif k == "p":
             parents()
@@ -548,29 +531,29 @@ def rank_program(g, core, T, topo):
             sent_notes(w + 1)
         elif k == "S":
             send(w + 1)
+        else:
+            step(t, w + 1)
 
     def step(t, w):
-        one = {"Q": gather, "E": spread, "s": compare, "C": count, "O": offsets, "X": scatter, "a": old_half, "G": ghosts, "g": into_table,
-               "M": marks, "H": scalar_table, "N": entries, "n": entries_turned}
+        one = {"Q": gather, "e": spread, "s": compare, "C": count, "O": offsets, "X": scatter, "a": old_half, "G": ghosts,
+               "i": into_table, "M": marks, "H": scalar_table, "h": narrow, "N": entries}
         k, n = t[0], int(t[1:])
         if k in one:
             one[k](n, w)
         elif k == "R":
-            if w + 1 < WAVES:
-                reset(n, w + 1)
+            if not last(w):
+                reset(w + 1)
         elif k == "f":
-            if w == 0 or n == 0:
-                pf([i for i in own if CH[i][0] // 4 == n] if w == 0 else own)
-        elif w == 0 and k == "K":
-            [late_gpsimd, vector_values, ghost_constants, late_scalar, late_vector, columns, lambda: fill(T.IV0[:, 0:3584:2], NONE, ["IV0"]),
-             lambda: reset(0, 0, 0, 896), lambda: reset(0, 0, 896, 1792), lambda: (sent_notes(0), send(0))][n]()
-        elif w == 0 and k == "P":
-            vcopy(T.P16[:, 32 * n:32 * n + 32], T.UPW[:, 448 * n:448 * n + 448].indirect(T.LISTC[:, 2 * n:2 * n + 2]),
-                  ["LISTC", "UPW%d" % n], ["P%d" % i for i in own if CH[i][0] // 4 == n])
+            pf([n] if w == 0 else [0, 1, 2, 3])
+        elif k == "K":
+            [first_lists, for_counts, vector_values, for_ghosts, for_turns, for_lists, for_sums, for_frontiers, no_offers,
+             lambda: reset(0, 0, 704), lambda: reset(0, 704, 1792), lambda: (sent_notes(0), send(0)), scales, ghost_fill][n]()
+        elif k == "P":
+            vcopy(T.P16[:, 32 * n:32 * n + 32], T.UPW[:, 448 * n:448 * n + 448].indirect(T.LISTC[:, 2 * n:2 * n + 2]), ["LISTC", "UPW%d" % n], ["P%d" % n])
 
     for w in range(WAVES):
         for t in (ORDER if w else FIRST).split():
             step(t, w)
-        for t in (TAIL if w + 1 < WAVES else LAST).split():
+        for t in (LAST if last(w) else TAIL).split():
             tail(t, w)
     finish([("lsem", engines[0] * WAVES)] + [("arr%d" % w, 4 * engines[0]) for w in range(WAVES)])

from concourse.bass import DstId, RemoteDMATransfer
from concourse.mybir import AluOpType, ActivationFunctionType

ALU = AluOpType
ACT = ActivationFunctionType
MAGIC = 8388608.0
HALF = 0.5 - 1.0 / 2048
WAVES = 4
ENT, NODE = 32, 192
NONE = 4096.0
STEP = 64
NA = 9
PIECES = [(32 * i, 32 * i + 32) for i in range(5)]
GATHER = "VAAAA"
GATHER0 = "AAAAA"
DBANK = ["D0", "D1", "S0", "S1", "D0"]
CBANK = ["Y0", "Y1", "Y0", "Y1", "Y0"]
NARROW = (3,)
FILL = 640
FIRST = ("K4 K7 K2 K0 K1 K11 N0 e2 e1 e0 K8 K12 P0 Q0 K9 K10 K3 K6 P1 f1 Q1 P2 s0 Q2 f0 C0 e3 s1 C1 f2 P3 Q3 O0 X0 X1 X2 s2 C2 M0 X3 f3 s3 O2 O1 X9 X10 "
         "a1 G0 K13 G1 G2 C3 a0 e4 a3 M1 X11 O3 G3 X12 Q4 s4 C4 X4 X5 X6 X7 X8 a2 H0 H1 H2 h3 H3 X13 X14 O4 X15 X16 X17 X18 X19 H4 K5 R0 i0")
ORDER = ("N0 f0 e2 e1 Q0 s0 C0 Q2 s2 C2 e3 Q1 s1 C1 Q3 O0 R0 i0 X0 X1 X2 X3 O2 X9 G0 s3 C3 a3 G1 X10 G2 Q4 X11 O3 O1 X4 X12 G3 X13 M1 a0 e4 s4 C4 a1 a2 "
         "X5 X6 X7 X8 H0 H1 H2 h3 H3 X14 X15 O4 X16 X17 X18 X19 H4")
TAIL = "x0 x1 m0 t0 t1 m1 t2 t3 F0 c0 l0 w0 b0 u0 l1 w2 w1 b1 b2 k0 L0 w3 b3 r0 r2 L1 L2 Z0 S0 e0 r1 p0 r3"
LAST = "x0 x1 m0 t0 t1 m1 t2 l0 w0 t3 l1 w3 w2 b0 w1 b3 r3 r0 b2 r2 b1 r1"
WQ, RQ = "AVAA", "VVAA"
WL, RL = "AVAV", "AVAV"
SLOT, MID = 64, 28

SCRATCH = {
    "UPW": ("sbuf", [128, 1920], "int32"),
    "UPG": ("sbuf", [128, 480], "int32"),
    "B0": ("sbuf", [128, 2240], "bfloat16"),
    "B1": ("sbuf", [128, 2240], "bfloat16"),
    "IA0": ("sbuf", [128, 4096], "float32"),
    "IA1": ("sbuf", [128, 4096], "float32"),
    "IV": ("sbuf", [128, 4096], "bfloat16"),
    "IH": ("sbuf", [128, 1792], "float16"),
    "SA": ("sbuf", [128, 2560], "float32"),
    "SV": ("sbuf", [128, 2560], "bfloat16"),
    "SC": ("sbuf", [128, 512], "bfloat16"),
    "R0": ("sbuf", [128, 256], "bfloat16"),
    "Q": ("sbuf", [128, 2560], "bfloat16"),
    "SG": ("sbuf", [128, 2560], "bfloat16"),
    "W": ("sbuf", [128, 1792], "float16"),
    "P16": ("sbuf", [128, 160], "uint16"),
    "Pf": ("sbuf", [128, 160], "float16"),
    "OFFS": ("sbuf", [128, 160], "uint16"),
    "LIST": ("sbuf", [128, 10], "uint16"),
    "LISTC": ("sbuf", [128, 8], "uint16"),
    "LISTG": ("sbuf", [128, 2], "uint16"),
    "L16": ("sbuf", [128, 112], "uint16"),
    "LA": ("sbuf", [128, 128], "float32"),
    "LX": ("sbuf", [128, 132, 4], "float16"),
    "GL": ("sbuf", [128, 16, SLOT], "bfloat16"),
    "THR": ("sbuf", [128, 128], "bfloat16"),
    "FT0": ("sbuf", [128, 128], "bfloat16"),
    "FT1": ("sbuf", [128, 128], "bfloat16"),
    "FT2": ("sbuf", [128, 128], "bfloat16"),
    "CUM": ("sbuf", [128, 4, 16, 2], "bfloat16"),
    "OKB": ("sbuf", [128, 4, 128, 2], "bfloat16"),
    "ONE": ("sbuf", [128, 528], "bfloat16"),
    "ID": ("sbuf", [128, 128], "bfloat16"),
    "IDF": ("sbuf", [128, 128], "float16"),
    "IDH": ("sbuf", [128, 128], "float16"),
    "IDO": ("sbuf", [128, 128], "bfloat16"),
    "ID2": ("sbuf", [128, 128], "float16"),
    "IDM": ("sbuf", [128, 128], "bfloat16"),
    "IDL": ("sbuf", [128, 128], "bfloat16"),
    "IDU": ("sbuf", [128, 128], "bfloat16"),
    "TRI": ("sbuf", [128, 128], "bfloat16"),
    "UPR": ("sbuf", [128, 128], "bfloat16"),
    "CM": ("sbuf", [128, 128], "bfloat16"),
    "G1": ("sbuf", [128, 8], "bfloat16"),
    "G2": ("sbuf", [128, 8], "bfloat16"),
    "BWV": ("sbuf", [128, 144], "bfloat16"),
    "SEL": ("sbuf", [128, 32], "bfloat16"),
    "SELF": ("sbuf", [128, 8], "float32"),
    "SELH": ("sbuf", [128, 8], "float16"),
    "IP": ("sbuf", [128, 1], "int32"),
    "IT": ("sbuf", [128, 2], "int32"),
    "COL": ("sbuf", [128, 16], "float32"),
    "BI": ("sbuf", [128, 20], "float32"),
    "WV": ("sbuf", [128, 8], "float32"),
    "RW": ("sbuf", [128, 96], "bfloat16"),
    "CI": ("sbuf", [128, 18], "int32"),
    "CL": ("sbuf", [128, 12], "bfloat16"),
    "CLf": ("sbuf", [128, 16], "float32"),
    "CG": ("sbuf", [128, 2], "bfloat16"),
    "FRI": ("sbuf", [128, 8], "int32"),
    "FRF": ("sbuf", [128, 8], "float32"),
    "LF": ("sbuf", [128, 16], "float32"),
}
for _w in range(WAVES):
    SCRATCH["NB%d" % _w] = ("sbuf", [128, 144], "bfloat16")
for _n in ("D0", "D1", "S0", "S1", "Y0", "Y1", "X0", "X1"):
    SCRATCH["ps" + _n] = ("psum", [128, 512], "float32")
SEMAPHORES = (["sv", "sa", "st", "sg", "lrec", "lfr", "lupg", "lsem"] + ["lup%d" % i for i in range(4)]
              + ["arr%d" % w for w in range(WAVES)] + ["out%d" % i for i in range(4)])
CSEM = {"V": "sv", "A": "sa", "T": "st", "G": "sg"}


def make_tracker(g, T):
    qs = {"V": g.vector, "A": g.scalar, "T": g.tensor, "G": g, "S": g.sync}
    known = {q: {} for q in qs}
    cnt, lw, rd, pa, seq = {}, {}, {}, {}, [0]

    def settle(q, evs):
        for ev in sorted(evs, key=lambda e: -e[4]):
            if known[q].get(ev[1], 0) >= ev[2]:
                continue
            qs[q].wait_ge(T.sem[ev[1]], ev[2])
            for s, v in ev[3].items():
                if known[q].get(s, 0) < v:
                    known[q][s] = v
            known[q][ev[1]] = ev[2]

    def op(q, call, R=(), W=(), sem=None, inc=1):
        tag = q if sem is None else "dma"
        evs = []
        for t in list(R) + list(W):
            if t[:2] == "ps":
                evs += [e for k, e in pa.get(t, {}).items() if k != tag]
        for t in R:
            if t[:2] != "ps":
                evs += lw.get(t, [])
        for t in W:
            if t[:2] != "ps":
                evs += lw.get(t, []) + list(rd.get(t, {}).values())
        settle(q, evs)
        s = CSEM[q] if sem is None else sem
        r = call(qs[q])
        for ins in (r if isinstance(r, list) else [r]):
            ins.then_inc(T.sem[s], inc)
            cnt[s] = cnt.get(s, 0) + inc
        seq[0] += 1
        ev = (tag, s, cnt[s], dict(known[q]), seq[0])
        for t in list(R) + list(W):
            if t[:2] == "ps":
                pa.setdefault(t, {})[tag] = ev
        for t in R:
            if t[:2] != "ps":
                rd.setdefault(t, {})[tag if tag != "dma" else s] = ev
        for t in W:
            if t[:2] != "ps":
                lw[t] = [ev]
                rd[t] = {}

    def arrive(t, sem, val):
        seq[0] += 1
        lw[t] = [("remote", sem, val, {}, seq[0])]

    def ready(q, toks):
        settle(q, [e for t in toks for e in lw.get(t, [])])

    def finish(extra):
        for s, v in list(cnt.items()) + extra:
            if known["G"].get(s, 0) < v:
                g.wait_ge(T.sem[s], v)
    return op, arrive, ready, finish


def rank_program(g, core, T, topo):
    rank = T.rank_of(core)
    if rank is None:
        return
    N = len(T.cores)
    op, arrive, ready, finish = make_tracker(g, T)
    name = lambda w: "B%d" % (w % 2)
    tab = lambda w: T[name(w)]
    nodes_of = lambda w: ["%sn%d" % (name(w), i) for i in range(4)]
    ents_of = lambda w: ["%se%d" % (name(w), i) for i in range(2)]
    nodes = lambda w, i: tab(w)[:, NODE + 448 * i:NODE + 448 * i + 448]
    col = lambda c: NODE - 1 - 8 * c
    lane = lambda b: 2 * (b % 2) + b % 4 // 2
    turned = lambda b: slice(32 * (b // 4) + lane(b), 32 * (b // 4) + 32, 4)
    last = lambda w: w + 1 == WAVES

    def vts(out, in0, s1, s2, op0, op1, R, W):
        if op1 is None:
            op("V", lambda v: v.tensor_scalar(out, in0, s1, None, op0), R, W)
        else:
            op("V", lambda v: v.tensor_scalar(out, in0, s1, s2, op0, op1), R, W)

    def vtt(out, in0, in1, o, R, W):
        op("V", lambda v: v.tensor_tensor(out, in0, in1, o), R, W)

    def vcopy(out, in_, R, W):
        op("V", lambda v: v.tensor_copy(out, in_), R, W)

    def fill(ap, c, W):
        op("V", lambda v: v.memset(ap, c), (), W)

    def sel(out, in_, pat, cmp, base, cm, R, W):
        op("G", lambda q: q.affine_select(out, in_, pat, cmp, 0.0, base, cm), R, W)

    def gcopy(out, in_, n, R, W):
        sel(out, in_, [[0, n]], ALU.is_gt, 1, 0, R, W)

    def iota(out, pat, base, cm, W):
        op("G", lambda q: q.iota(out, pat, base, cm), (), W)

    def iotaf(out, pat, base, cm, W):
        op("G", lambda q: q.iota(out, pat, base, cm, allow_small_or_imprecise_dtypes=True), (), W)

    def act(out, in_, R, W, scale=1.0, bias=None, f=None):
        if bias is None:
            op("A", lambda a: a.activation(out, in_, f or ACT.Copy, scale=scale), R, W)
        else:
            op("A", lambda a: a.activation(out, in_, f or ACT.Identity, bias=bias, scale=scale), R, W)

    def copy(q, out, in_, R, W):
        (vcopy if q == "V" else act)(out, in_, R, W)

    def mm(calls, R, W):
        op("T", lambda t: [t.matmul(*c) for c in calls], R, W)

    op("S", lambda s: s.dma_start(T.FRI[:, :], T.fr[:, :]), (), ["FRI"], "lfr", 16)
    op("A", lambda s: s.dma_start(T.B0[:, NODE:NODE + 1792], T.rec[:, :]), (), nodes_of(0), "lrec", 16)
    for i in range(4):
        op("S", lambda s: s.dma_start(T.UPW[:, 448 * i:448 * i + 448], T.up[:, 448 * i:448 * i + 448]),
           (), ["UPW%d" % i], "lup%d" % i, 16)
    op("S", lambda s: [s.dma_start(T.UPG[:, 120 * d:120 * d + 112], T.up[:, 1792 + 112 * d:1904 + 112 * d]) for d in range(4)],
       (), ["UPG"], "lupg", 16)

    C = lambda i: T.COL[:, i:i + 1]

    fill(T.ONE[:, :], 1.0, ["ONE"])
    iota(T.IP[:, :], [[0, 1]], 0, 1, ["IP"])
    iota(T.CI[:, 0:8], [[224, 8]], 0, 0, ["CI0"])
    iota(T.CI[:, 8:16], [[0, 4], [224, 2]], 0, 0, ["CI1"])
    iotaf(T.R0[:, :], [[1, 16], [0, 16]], ENT, 0, ["R0"])
    iotaf(T.BI[:, :], [[-8, 20]], col(0) + ENT, 0, ["BI"])
    sel(T.ID[:, :], T.ONE[:, 0:128], [[-1, 128]], ALU.is_equal, 0, 1, ["ONE"], ["ID"])
    sel(T.G1[:, :], T.ONE[:, 0:8], [[-16, 8]], ALU.is_ge, 0, 1, ["ONE"], ["G1"])
    sel(T.G2[:, :], T.G1[:, :], [[16, 8]], ALU.is_ge, 14, -1, ["G1"], ["G2"])
    act(T.B1[:, NODE + 1792:2240], T.ONE[:, 0:256], ["ONE"], ["B1z"], 0.0, None, ACT.Silu)
    for b in range(0, NA, 2):
        n = 128 * min(2, NA - b)
        act(T.SA[:, 128 * b:128 * b + n], T.R0[:, 0:n], ["R0", "BI"], ["SA%d" % b], -1.0, T.BI[:, b:b + 1])
    vts(T.IT[:, 1:2], T.IP[:, :], 3, 1, ALU.logical_shift_right, ALU.bitwise_and, ["IP"], ["IT1"])
    vts(T.IT[:, 0:1], T.IP[:, :], 15, None, ALU.bitwise_and, None, ["IP"], ["IT0"])
    vts(C(3), T.IT[:, 1:2], 112.0, None, ALU.mult, None, ["IT1"], ["c3"])
    vts(C(0), T.IT[:, 0:1], 14.5, None, ALU.is_lt, None, ["IT0"], ["c0"])
    vts(T.CLf[:, 0:8], T.CI[:, 0:8], C(3), None, ALU.add, None, ["CI0", "c3"], ["CLf0"])
    vts(C(1), C(0), -2.0, 2.0, ALU.mult, ALU.add, ["c0"], ["c1"])
    vts(T.CLf[:, 8:16], T.CI[:, 8:16], C(3), None, ALU.add, None, ["CI1", "c3"], ["CLf1"])

    def places(w, src, tok):
        vcopy(T["NB%d" % w][:, 14:16], src, [tok], ["NBp%d" % w])

    def first_lists():
        vcopy(T.FRF[:, :], T.FRI[:, :], ["FRI"], ["FRF"])
        places(0, T.FRI[:, 0:2], "FRI")
        vtt(T.LF[:, 0:8], T.FRF[:, :], T.CLf[:, 0:8], ALU.add, ["FRF", "CLf0"], ["LF0"])
        vtt(T.LF[:, 8:16], T.FRF[:, :], T.CLf[:, 8:16], ALU.add, ["FRF", "CLf1"], ["LF1"])
        vcopy(T.LIST[:, 0:8], T.LF[:, 0:8], ["LF0"], ["LIST"])
        vcopy(T.LISTC[:, :], T.LF[:, 8:16], ["LF1"], ["LISTC"])

    def reset(w, lo=0, hi=1792):
        iotaf(T["IA%d" % (w % 2)][:, 2 * lo:2 * hi:2], [[1, hi - lo]], NODE + lo, 0, ["IA%d" % (w % 2)])

    def for_counts():
        fill(T.B0[:, NODE + 1792:2240], 0.0, ["B0z"])
        fill(T.BWV[:, :], 0.0, ["BWV"])
        vts(T.ID2[:, :], T.ID[:, :], 2.0, None, ALU.mult, None, ["ID"], ["ID2"])
        vts(T.BWV[:, 15:128:16], T.G2[:, :], -1.0 / 16, None, ALU.mult, None, ["G2", "BWV"], ["BWV"])

    def vector_values():
        for b in range(NA, 20, 2):
            n = 128 * min(2, 20 - b)
            vts(T.SV[:, 128 * b:128 * b + n], T.R0[:, 0:n], -1.0, float(col(b) + ENT), ALU.mult, ALU.add, ["R0"], ["SV%d" % b])

    def for_ghosts():
        vcopy(C(2), T.IT[:, 1:2], ["IT1"], ["c2"])
        vts(C(5), T.IT[:, 1:2], -1.0, 1.0, ALU.mult, ALU.add, ["IT1"], ["c5"])
        vts(T.CG[:, 0:1], T.IT[:, 1:2], 120.0, None, ALU.mult, None, ["IT1"], ["CG0"])
        vts(T.CG[:, 1:2], T.IT[:, 1:2], 120.0, 240.0, ALU.mult, ALU.add, ["IT1"], ["CG1"])
        fill(C(11), float(NODE), ["c11"])
        vts(T.IDL[:, :], T.ID[:, :], C(5), None, ALU.mult, None, ["ID", "c5"], ["IDL"])
        vts(T.IDU[:, :], T.ID[:, :], C(2), None, ALU.mult, None, ["ID", "c2"], ["IDU"])

    def ghost_fill():
        for d in range(4):
            iota(T.UPG[:, 120 * d + 112:120 * d + 120], [[16, 8]], 1792, 1, ["UPGp%d" % d])

    def for_turns():
        for t in ("SEL", "SELF", "SELH"):
            sel(T[t][:, 0:8], T.ONE[:, 0:8], [[-16, 8]], ALU.is_equal, -15, 1, ["ONE"], [t + "0" * (t == "SEL")])

    def for_lists():
        iota(T.UPW[:, 1792:1920], [[0, 8], [16, 16]], 1792, 1, ["UPWp"])
        sel(T.TRI[:, :], T.ONE[:, 0:128], [[1, 128]], ALU.is_ge, 0, -1, ["ONE"], ["TRI"])
        sel(T.LX[:, :, :], T.ONE[:, :], [[0, 528]], ALU.is_gt, 0, 0, ["ONE"], ["LXz"])
        iotaf(T.UPR[0:1, 112:120], [[1, 8]], 1, 0, ["UPR"])
        for t in ("B0", "B1"):
            sel(T[t][:, 0:ENT], T.ONE[:, 0:ENT], [[0, ENT]], ALU.is_gt, 0, 0, ["ONE"], [t + "y"])

    def for_sums():
        for t, c in (("IDO", 0.5), ("IDH", HALF), ("IDM", -float(NODE)), ("IDF", 1.0)):
            vts(T[t][:, :], T.ID[:, :], c, None, ALU.mult, None, ["ID"], [t])
        vts(T.CM[0:2, :], T.ONE[0:2, 0:128], T.COL[0:2, 13:14], None, ALU.mult, None, ["ONE", "c13"], ["CM"])
        vcopy(T.CL[:, 0:8], T.CLf[:, 0:8], ["CLf0"], ["CL0"])
        vcopy(T.CL[:, 8:10], T.CLf[:, 0:2], ["CLf0"], ["CL1"])
        fill(T.CL[:, 10:12], 0.0, ["CL2"])

    def for_frontiers():
        vts(C(7), T.IP[:, :], 120.0, None, ALU.is_equal, None, ["IP"], ["c7"])
        vts(T.WV[:, :], T.CI[:, 0:8], -1.0, 1679.0, ALU.mult, ALU.add, ["CI0"], ["WV"])
        fill(T.RW[:, :], 0.0, ["RW"])
        vts(C(13), T.IP[:, :], -MAGIC - 128.0, MAGIC, ALU.mult, ALU.add, ["IP"], ["c13"])
        vts(T.RW[:, 0:96:13], T.WV[:, :], C(7), 1.0, ALU.mult, ALU.add, ["WV", "c7", "RW"], ["RW"])
        fill(C(8), -MAGIC, ["c8"])
        vts(T.RW[:, 10:24:13], T.ONE[:, 0:2], C(7), None, ALU.subtract, None, ["ONE", "c7", "RW"], ["RW"])
        fill(C(12), 256.0, ["c12"])
        vts(T.RW[:, 8:22:13], T.RW[:, 10:24:13], 113.0, -112.0, ALU.mult, ALU.add, ["RW"], ["RW"])
        fill(T.UPR[0:1, :], 0.0, ["UPR"])

    def no_offers():
        fill(C(14), NONE, ["c14"])
        fill(T.IV[:, 0:2 * FILL:2], NONE, ["IV"])
        act(T.IV[:, 2 * FILL:3584:2], T.SA[:, 0:1792 - FILL], ["c14"] + ["SA%d" % b for b in range(0, NA, 2)], ["IVa"], 0.0, C(14))

    def scales():
        for w in range(1, WAVES):
            fill(T.SC[:, 128 * w:128 * w + 128], 1.0 / STEP ** w, ["SC%d" % w])
            vts(T.SEL[:, 8 * w:8 * w + 8], T.SEL[:, 0:8], float(STEP ** w), None, ALU.mult, None, ["SEL0"], ["SEL%d" % w])

    def marks(n, w):
        if n == 0:
            mm([(T.psX1[0:112, turned(b)], tab(w)[:, NODE + 112 * b:NODE + 112 * b + 112], T.SEL[:, 0:8], True, True) for b in range(16)],
               nodes_of(w) + ["SEL0"], ["psX1"])
            act(T.THR[0:112, :], T.psX1[0:112, 0:128], ["psX1", "c11"], ["THR"], -float(NODE), T.COL[0:112, 11:12])
        elif not last(w):
            o = T.psX0[0:112, 128:256]
            mm([(o, T.ID[0:112, 0:112], T.THR[0:112, :], True, w == 0)]
               + [(o, T.IDM[0:112, 0:112], T["FT%d" % k][0:112, :], False, k == w - 1) for k in range(w)],
               ["ID", "IDM", "THR"] + ["FT%d" % k for k in range(w)], ["psX0"])

    def entry_notes(i, w):
        if i == 4:
            return T.GL[:, 4 * w:4 * w + 4, MID:MID + 8], ["GL%d" % w]
        return T["NB%d" % w][:, 16 + 32 * i:48 + 32 * i], ["NB%s%d" % ("n" if i else "z", w)]

    def window(w):
        return tab(w)[:, NODE:2240], nodes_of(w) + [name(w) + "z"]

    def gather(i, w):
        (a, b), (win, R) = PIECES[i], window(w)
        copy((GATHER if w else GATHER0)[i], T.Q[:, 16 * a:16 * b], win.indirect(T.P16[:, a:b]), R + ["P%d" % (a // 32)], ["Q%d" % i])

    def spread(i, w):
        src, R = entry_notes(i, w)
        ps = "ps" + DBANK[i]
        mm([(T[ps][:, t:512:16], T.ID[:, :], src, True, True) for t in range(16)], R + ["ID"], [ps])

    def compare(i, w):
        a, b = PIECES[i]
        ps, x = "ps" + DBANK[a // 32], 16 * (a % 32)
        vtt(T.SG[:, 16 * a:16 * b], T.Q[:, 16 * a:16 * b], T[ps][:, x:x + 16 * (b - a)], ALU.is_ge, [ps, "Q%d" % i], ["SG%d" % i])

    def count(i, w):
        (a, b), ps = PIECES[i], "ps" + CBANK[i]
        out = T[ps][:, a:b]
        mm([(out, T.ID2[:, :], T.Pf[:, a:b], True, False)]
           + [(out, T.BWV[:, 15 - k:143 - k], T.SG[:, 16 * a + k:16 * b:16], False, k == 15) for k in range(16)],
           ["ID2", "BWV", "Pf%d" % (a // 32), "SG%d" % i], [ps])

    def offsets(i, w):
        (a, b), ps = PIECES[i], "ps" + CBANK[i]
        vts(T.OFFS[:, a:b], T[ps][:, a:b], 1.03125, None, ALU.add, None, [ps], ["OF%d" % i])

    def scatter(c, w):
        off = T.OFFS[:, 8 * c:8 * c + 8]
        R = ["OF%d" % i for i, (a, b) in enumerate(PIECES) if a <= 8 * c < b]
        if c < NA:
            t = "IA%d" % (w % 2)
            op("A", lambda a: a.activation(T[t][:, :].indirect(off), T.SA[:, 128 * c:128 * c + 128], ACT.Silu), R + ["SA%d" % (c // 2 * 2)], [t])
        elif w == 0:
            vcopy(T.IV[:, :].indirect(off), T.SV[:, 128 * c:128 * c + 128], R + ["SV%d" % (c - (c - NA) % 2), "IVa"], ["IV"])
        else:
            vtt(T.IV[:, :].indirect(off), T.SV[:, 128 * c:128 * c + 128], T.SC[:, 128 * w:128 * w + 128], ALU.mult, R + ["SC%d" % w], ["IV"])

    def turn_table(t, s, step, ps, quarters, w=0):
        mm([(T[ps][0:112, turned(b)], T[t][:, step * 112 * b:step * 112 * (b + 1):step], T[s][:, 8 * w:8 * w + 8], True, True)
            for b in range(4 * quarters[0], 4 * quarters[-1] + 4)], [t if step == 2 else "IH%d" % quarters[0], s + str(w) * (s == "SEL")], [ps])

    def narrow(i, w):
        t = "IA%d" % (w % 2)
        if i in NARROW:
            act(T.IH[:, 448 * i:448 * i + 448], T[t][:, 896 * i:896 * i + 896:2], [t], ["IH%d" % i])

    def scalar_table(n, w):
        if n == 4:
            vcopy(T.LA[0:112, :], T.psX1[0:112, 0:128], ["psX1"], ["LA"])
        elif n in NARROW:
            turn_table("IH", "SELH", 1, "psX1", [n])
        else:
            turn_table("IA%d" % (w % 2), "SELF", 2, "psX1", [n])

    def pf(ks):
        a, b = 32 * ks[0], 32 * ks[-1] + 32
        vcopy(T.Pf[:, a:b], T.P16[:, a:b], ["P%d" % k for k in ks], ["Pf%d" % k for k in ks])

    def parents():
        vcopy(T.P16[:, 0:128], T.UPW[:, :].indirect(T.LIST[:, 0:8]), ["LIST", "UPWp"] + ["UPW%d" % i for i in range(4)], ["P%d" % k for k in range(4)])

    start = lambda d: MID - 2 - 8 * d

    def send(w):
        dst = [T.cores[(rank + d) % N] for d in range(1, 5)]
        common = [e for e in topo.engines(core, dst[0]) if all(e in topo.engines(core, c) for c in dst)]
        ne = max(x for x in (1, 2, 4, 8, 16) if x <= len(common))
        m = sum(1 << e for e in common[:ne])
        ids = []
        for c in dst:
            rid, pid = topo.addr(c, core)
            ids.append(DstId(rid=rid, pnc=pid))
        ready("G", ["NBz%d" % w, "NBp%d" % w])
        g.remote_dma_fused([RemoteDMATransfer(
            dst_ids=ids, dma_engine_mask=m, remote_sem=T.sem["arr%d" % w], srcs=[T["NB%d" % w][:, 14:48]],
            dsts=[T.GL[:, 4 * w + d, start(d):start(d) + 34] for d in range(4)])], local_sem=T.sem["lsem"])
        arrive("GL%d" % w, "arr%d" % w, 4 * ne)
        engines[0] = ne

    engines = [0]

    def sent_notes(w):
        x = 8 if w else 0
        vts(T["NB%d" % w][:, 16:48], tab(w)[:, NODE:NODE + 448].indirect(T.LIST[:, x:x + 2]), C(0), C(1), ALU.mult, ALU.add,
            nodes_of(w)[:1] + ["LIST", "c0", "c1"], ["NBz%d" % w])

    def entries(n, w):
        win, R = window(w)
        act(T["NB%d" % w][:, 48:144], win.indirect(T.LIST[:, 2:8]), R + ["LIST", "c0", "c1"], ["NBn%d" % w], C(0), C(1))

    def ghosts(n, w):
        if n == 0:
            place = lambda d: T.GL[:, 4 * w + d, start(d) + d // 2:start(d) + 1 + d // 2]
            mm([(T.psX0[:, 0:2], T.ID[:, :], T.CG[:, :], True, False)]
               + [(T.psX0[:, d // 2:d // 2 + 1], T[("IDL", "IDU")[d % 2]][:, :], place(d), False, d == 3) for d in range(4)],
               ["ID", "IDL", "IDU", "CG0", "CG1", "GL%d" % w], ["psX0"])
        elif n == 1:
            vcopy(T.LISTG[:, :], T.psX0[:, 0:2], ["psX0"], ["LISTG"])
        elif n == 2:
            vcopy(T.P16[:, 128:160], T.UPG[:, :].indirect(T.LISTG[:, :]), ["LISTG", "UPG"] + ["UPGp%d" % d for d in range(4)], ["P4"])
        else:
            pf([4])

    def into_table(n, w):
        e = ents_of(w)
        gcopy(tab(w)[:, col(0):col(16):-1], T["NB%d" % w][:, 16:144], 128, ["NBn%d" % w, "NBz%d" % w], [e[0]])
        gcopy(tab(w)[:, col(16):col(20):-1], entry_notes(4, w)[0], 32, ["GL%d" % w], [e[1]])

    SUM = ["psS0", "psS1", "psD0", "psD1"]
    LEAST = ["psX0", "psY0"]
    TURN = ["psY1", "psX1"]
    rounder = lambda i, w: (RL if last(w) else RQ)[i]

    def turn_list(i, w):
        ps = TURN[i // 2]
        mm([(T[ps][:, 28 * i:28 * i + 28], T.LX[0:112, 32 * i + 3 - r:32 * i + 35 - r, :], T.IDF[0:112, r:112:4], r == 0, r == 3) for r in range(4)],
           ["LX%d" % (i // 2), "IDF"], [ps])

    def winners(i, w):
        out, win = T.W[:, 448 * i:448 * i + 448], tab(w)[:, 0:NODE + 1792].indirect(T.L16[:, 28 * i:28 * i + 28])
        R = nodes_of(w) + ents_of(w) + [name(w) + "y", "L16%d" % i]
        if (WL if last(w) else WQ)[i] == "V":
            vts(out, win, 256.0, None, ALU.add, None, R, ["W%d" % i])
        else:
            act(out, win, R + ["c12"], ["W%d" % i], 1.0, C(12))

    def old_half(i, w):
        o = T[SUM[i]][:, 0:448]
        mm([(o, T.CM[0:2, :], T.ONE[0:2, 0:448], True, False)] * (rounder(i, w) == "A")
           + [(o, T.IDO[:, :], nodes(w, i), rounder(i, w) == "V", False)], ["IDO", "CM", "ONE", nodes_of(w)[i]], [SUM[i]])

    def new_half(i, w):
        ps = T[SUM[i]]
        mm([(ps[:, 112 * j:112 * j + 112], T.IDH[:, :], T.W[:, 448 * i + lane(j):448 * i + 448:4], False, j == 3) for j in range(4)],
           ["IDH", "W%d" % i], [SUM[i]])

    def round_down(i, w):
        out, tok, o = nodes(w + 1, i), nodes_of(w + 1)[i], T[SUM[i]][:, 0:448]
        if rounder(i, w) == "V":
            vts(out, o, MAGIC - 128.0, -MAGIC, ALU.add, ALU.add, [SUM[i]], [tok])
        else:
            act(out, o, [SUM[i], "c8"], [tok], 1.0, C(8))
        if last(w):
            op("S", lambda s: s.dma_start(T.y[:, 448 * i:448 * i + 448], out), [tok], ["y%d" % i], "out%d" % i, 16)

    def tail(t, w):
        k, n = t[0], int(t[1:])
        if k == "x":
            turn_table("IV", "SEL", 2, LEAST[n], [2 * n, 2 * n + 1], w)
        elif k == "m":
            vtt(T.LX[0:112, 64 * n + 3:64 * n + 67:4, :], T[LEAST[n]][0:112, 64 * n:64 * n + 64], T.LA[0:112, 64 * n:64 * n + 64], ALU.min,
                [LEAST[n], "LA", "LXz"], ["LX%d" % n])
        elif k == "t":
            turn_list(n, w)
        elif k == "l":
            vcopy(T.L16[:, 56 * n:56 * n + 56], T[TURN[n]][:, 56 * n:56 * n + 56], [TURN[n]], ["L16%d" % (2 * n), "L16%d" % (2 * n + 1)])
        elif k == "w":
            winners(n, w)
        elif k == "b":
            new_half(n, w)
        elif k == "r":
            round_down(n, w)
        elif k == "F":
            vtt(T["FT%d" % w][0:112, :], T.LX[0:112, 3:131:4, :], T.psX0[0:112, 128:256], ALU.is_lt, ["LX0", "LX1", "psX0"], ["FT%d" % w])
        elif k == "c":
            o = T.psY0[0:121, 0:128]
            mm([(o, T.UPR[0:1, 0:121], T.ONE[0:1, 0:128], True, False), (o, T.TRI[0:112, 0:121], T["FT%d" % w][0:112, :], False, True)],
               ["TRI", "UPR", "ONE", "FT%d" % w], ["psY0"])
        elif k == "u":
            vcopy(T.CUM[0:121, :, :, :], T.psY0[0:121, 0:128], ["psY0"], ["CUM"])
        elif k == "k":
            for j in range(8):
                vts(T.OKB[0:121, :, j:128:8, :], T.CUM[0:121, :, :, :], j + 0.5, None, ALU.is_lt, None, ["CUM"], ["OK%d" % j])
        elif t == "L0":
            mm([(T.psX0[:, 0:12], T.ID[:, :], T.CL[:, :], True, False)]
               + [(T.psX0[:, 0:12], T.OKB[0:121, c // 2, :, c % 2], T.RW[0:121, 12 * c:12 * c + 12], False, c == 7) for c in range(8)],
               ["ID", "CL0", "CL1", "CL2", "RW"] + ["OK%d" % j for j in range(8)], ["psX0"])
        elif t == "L1":
            vcopy(T.LIST[:, :], T.psX0[:, 0:10], ["psX0"], ["LIST"])
        elif t == "L2":
            places(w + 1, T.psX0[:, 10:12], "psX0")
        elif k == "p":
            parents()
        elif k == "Z":
            sent_notes(w + 1)
        elif k == "S":
            send(w + 1)
        else:
            step(t, w + 1)

    def step(t, w):
        one = {"Q": gather, "e": spread, "s": compare, "C": count, "O": offsets, "X": scatter, "a": old_half, "G": ghosts,
               "i": into_table, "M": marks, "H": scalar_table, "h": narrow, "N": entries}
        k, n = t[0], int(t[1:])
        if k in one:
            one[k](n, w)
        elif k == "R":
            if not last(w):
                reset(w + 1)
        elif k == "f":
            pf([n] if w == 0 else [0, 1, 2, 3])
        elif k == "K":
            [first_lists, for_counts, vector_values, for_ghosts, for_turns, for_lists, for_sums, for_frontiers, no_offers,
             lambda: reset(0, 0, 704), lambda: reset(0, 704, 1792), lambda: (sent_notes(0), send(0)), scales, ghost_fill][n]()
        elif k == "P":
            vcopy(T.P16[:, 32 * n:32 * n + 32], T.UPW[:, 448 * n:448 * n + 448].indirect(T.LISTC[:, 2 * n:2 * n + 2]), ["LISTC", "UPW%d" % n], ["P%d" % n])

    for w in range(WAVES):
        for t in (ORDER if w else FIRST).split():
            step(t, w)
        for t in (LAST if last(w) else TAIL).split():
            tail(t, w)
    finish([("lsem", engines[0] * WAVES)] + [("arr%d" % w, 4 * engines[0]) for w in range(WAVES)])
